import numpy as np
import ml_dtypes


def mxq(x, axis, fmt="e4m3"):
    dtype, down = {"e4m3": (ml_dtypes.float8_e4m3fn, 7), "e5m2": (ml_dtypes.float8_e5m2, 14)}[fmt]
    v = np.moveaxis(np.asarray(x, np.float32).astype(ml_dtypes.bfloat16).astype(np.float64), axis, -1)
    blocks = v.reshape(v.shape[:-1] + (-1, 32))
    amax = np.abs(blocks).max(-1, keepdims=True)
    byte = np.maximum(np.where(amax > 0, np.frexp(amax)[1] - 1 + 127, 0) - down, 1)
    scale = np.exp2(byte - 127.0)
    codes = (blocks / scale).astype(np.float32).astype(dtype).astype(np.float64)
    return np.moveaxis((codes * scale).reshape(v.shape), -1, axis)


WIDE = False


def mx_kscale(k):
    if not WIDE:
        return np.ones(k)
    levels = np.array([10, -10, 5, -5, 0])
    if k % 512:
        return np.exp2(np.random.permutation(np.resize(levels, k // 32))).repeat(32)
    a = np.empty((k // 512, 16))
    for p in range(k // 512):
        a[p, :8] = np.random.permutation(np.resize(levels, 8))
        for g in range(8):
            far = levels[np.abs(levels - a[p, g]) >= 10]
            a[p, g + 8] = far[np.random.randint(len(far))]
    return np.exp2(a.ravel()).repeat(32)


def f64(x):
    return np.asarray(x).astype(np.float64)


def striped(idx):
    return np.tile(idx.reshape(-1, 16).T, (8, 1)).astype(np.uint16)


def unstriped(offs):
    return offs[:16].T.reshape(-1).astype(np.int64)


def silu(v):
    return v / (1.0 + np.exp(-np.maximum(v, -700.0)))


K, T, E, C, H, N = 1024, 640, 5, 256, 512, 256


def by_expert(wq, xq):
    return np.concatenate([wq[e].T @ xq[:, e * C:(e + 1) * C] for e in range(E)], axis=1)


def setup_inputs():
    n = np.random.standard_normal
    s = mx_kscale(K)[:, None]
    u = mx_kscale(H)
    first = np.random.permutation(np.repeat(np.arange(E), T // E))
    second = (first + 1 + np.random.permutation(np.repeat(np.arange(E - 1), -(-T // (E - 1)))[:T])) % E
    while np.bincount(second, minlength=E).max() != T // E:
        load = np.bincount(second, minlength=E); hi, lo = int(load.argmax()), int(load.argmin())
        t = np.flatnonzero((second == hi) & (first != lo))[0]; second[t] = lo
    slot_token = np.empty(E * C, np.int64); pos = np.empty((2, T), np.int64); fill = np.zeros(E, np.int64)
    place = np.stack([np.random.permutation(C) for _ in range(E)])
    for r, deal in enumerate((first, second)):
        for t in np.random.permutation(T):
            e = deal[t]; j = e * C + place[e, fill[e]]; fill[e] += 1; slot_token[j] = t; pos[r, t] = j
    g = np.random.uniform(0.2, 0.8, T)
    w_slot = np.empty(E * C); w_slot[pos[0]] = g; w_slot[pos[1]] = 1.0 - g
    return {
        "xT": (n((K, T)) * s).astype(np.float32),
        "w1": (n((E, K, H)) / np.sqrt(K) / s[None]).astype(np.float32),
        "w3": (n((E, K, H)) / np.sqrt(K) / s[None] * u[None, None, :]).astype(np.float32),
        "w2": (n((E, H, N)) / np.sqrt(H) / u[None, :, None]).astype(np.float32),
        "gate": np.tile(w_slot, (K, 1)).astype(np.float32),
        "offs": striped(slot_token),
        "pos1": striped(pos[0]),
        "pos2": striped(pos[1]),
    }


def reference(xT, w1, w3, w2, gate, offs, pos1, pos2):
    idx = unstriped(offs)
    xq = mxq(f64(gate) * f64(xT)[:, idx], 0, "e4m3")
    h = silu(by_expert(mxq(f64(w1), 1, "e4m3"), xq))
    h = h * by_expert(mxq(f64(w3), 1, "e4m3"), xq)
    y = by_expert(mxq(f64(w2), 1, "e4m3"), mxq(h, 0, "e4m3"))
    return y[:, unstriped(pos1)] + y[:, unstriped(pos2)]

@@ -1,0 +1,193 @@
+from contextlib import ExitStack
+
+import concourse.mybir as mybir
+
+K, T, E, C, H, N = 1024, 640, 5, 256, 512, 256
+S = E * C
+P = 128
+PACK = 4
+K_PASS = P * PACK
+PASSES = K // K_PASS
+HALF = 128
+
+FLOPS = 2 * S * (2 * K * H + H * N)
+BYTES = 4 * (K * T + E * (2 * K * H + H * N) + S + N * T) + 2 * P * (S + 2 * T) // 16
+
+F32 = mybir.dt.float32
+BF16 = mybir.dt.bfloat16
+U32 = mybir.dt.uint32
+U16 = mybir.dt.uint16
+U8 = mybir.dt.uint8
+FP8X4 = mybir.dt.float8_e4m3fn_x4
+MULT = mybir.AluOpType.mult
+ADD = mybir.AluOpType.add
+SILU = mybir.ActivationFunctionType.Silu
+
+ORDER = [('lo',), ('lg', 0), ('lx', 0, 0), ('lx', 0, 1), ('lg', 1), ('lw', 0, 0, 0), ('lx', 0, 2), ('lw', 0, 0, 1), ('lw', 0, 1, 0), ('lx', 0, 3), ('lw', 0, 1, 1), ('lx', 1, 0), ('lw', 1, 0, 0), ('lx', 1, 1), ('lx', 1, 2), ('lw', 1, 0, 1), ('lw', 1, 1, 0), ('lw', 1, 1, 1), ('lx', 1, 3), ('lw', 2, 0, 0), ('lw', 2, 0, 1), ('lw', 2, 1, 0), ('lw', 2, 1, 1), ('lw', 3, 0, 0), ('lw', 3, 0, 1), ('lw', 3, 1, 0), ('lw', 3, 1, 1), ('lw', 4, 0, 0), ('lw', 4, 0, 1), ('lw', 4, 1, 0), ('lw', 4, 1, 1), ('lw2', 0), ('lw2', 1), ('lw2', 2), ('lw2', 3), ('lp',), ('lw2', 4), ('G', 0, 1, 0, 0), ('G', 1, 3, 0, 0), ('G', 0, 1, 0, 1), ('G', 1, 3, 0, 1), ('G', 0, 1, 0, 2), ('cw', 0, 0, 0, None, 'S'), ('G', 1, 3, 0, 2), ('G', 3, 5, 0, 0), ('G', 0, 1, 0, 3), ('cw', 0, 0, 1, None, 'S'), ('G', 1, 3, 0, 3), ('G', 3, 5, 0, 1), ('G', 0, 1, 1, 0), ('cw', 0, 1, 0, None, 'S'), ('G', 1, 3, 1, 0), ('qw', 0, 0, 0), ('G', 3, 5, 0, 2), ('cw', 0, 1, 1, None, 'S'), ('G', 0, 1, 1, 1), ('G', 1, 3, 1, 1), ('qw', 0, 0, 1), ('G', 3, 5, 0, 3), ('cw', 1, 0, 0, None, 'S'), ('G', 0, 1, 1, 2), ('G', 1, 3, 1, 2), ('qw', 0, 1, 0), ('cw', 1, 0, 1, None, 'S'), ('G', 3, 5, 1, 0), ('G', 0, 1, 1, 3), ('G', 1, 3, 1, 3), ('qw', 0, 1, 1), ('cw', 1, 1, 0, None, 'S'), ('G', 3, 5, 1, 1), ('qw', 1, 0, 0), ('cx', 0, 0, 'S'), ('cw', 1, 1, 1, None, 'S'), ('G', 3, 5, 1, 2), ('cx', 1, 0, 'V'), ('qw', 1, 0, 1), ('cx', 0, 1, 'S'), ('qx', 0, 0), ('cw', 2, 0, 0, 0, 'S'), ('cw', 2, 0, 0, 1, 'V'), ('cx', 2, 0, 'S'), ('G', 3, 5, 1, 3), ('cw2', 0, 'V'), ('qx', 1, 0), ('qw', 1, 1, 0), ('qx', 0, 1), ('mm', 0, 0, 0), ('mm', 0, 0, 1), ('mm', 0, 1, 0), ('mm', 0, 1, 1), ('cx', 1, 1, 'S'), ('cx', 3, 0, 'S'), ('qw2', 0), ('cw', 2, 0, 1, None, 'S'), ('qx', 2, 0), ('silu', 0, 0), ('silu', 0, 1), ('cx', 4, 0, 'S'), ('qw', 1, 1, 1), ('qx', 1, 1), ('h', 0, 0), ('h', 0, 1), ('mm', 1, 0, 0), ('mm', 1, 0, 1), ('mm', 1, 1, 0), ('mm', 1, 1, 1), ('qx', 3, 0), ('cx', 2, 1, 'S'), ('cw', 2, 1, 0, None, 'V'), ('qh', 0), ('mmy', 0), ('silu', 1, 0), ('silu', 1, 1), ('qw', 2, 0, 0), ('qx', 4, 0), ('cy', 0), ('qx', 2, 1), ('h', 1, 0), ('h', 1, 1), ('cw', 2, 1, 1, 0, 'S'), ('cw', 2, 1, 1, 1, 'V'), ('cx', 3, 1, 'V'), ('qh', 1), ('qw', 2, 0, 1), ('mm', 2, 0, 0), ('mm', 2, 0, 1), ('cw', 3, 0, 0, 0, 'S'), ('cw', 3, 0, 0, 1, 'V'), ('silu', 2, 0), ('silu', 2, 1), ('qx', 3, 1), ('cx', 4, 1, 'S'), ('qw', 2, 1, 0), ('cw', 3, 0, 1, 0, 'S'), ('cw', 3, 0, 1, 1, 'V'), ('qx', 4, 1), ('qw', 2, 1, 1), ('mm', 2, 1, 0), ('mm', 2, 1, 1), ('cw', 3, 1, 0, 0, 'S'), ('cw', 3, 1, 0, 1, 'V'), ('h', 2, 0), ('h', 2, 1), ('qw', 3, 0, 0), ('qh', 2), ('cw', 3, 1, 1, None, 'S'), ('qw', 3, 0, 1), ('mm', 3, 0, 0), ('mm', 3, 0, 1), ('cw', 4, 0, 0, 0, 'S'), ('cw', 4, 0, 0, 1, 'V'), ('cw2', 1, 'V'), ('silu', 3, 0), ('silu', 3, 1), ('qw', 3, 1, 0), ('qw2', 1), ('mmy', 1), ('cw', 4, 0, 1, None, 'V'), ('cy', 1), ('qw', 3, 1, 1), ('mm', 3, 1, 0), ('mm', 3, 1, 1), ('cw', 4, 1, 0, None, 'S'), ('h', 3, 0), ('h', 3, 1), ('qw', 4, 0, 0), ('qh', 3), ('cw', 4, 1, 1, None, 'V'), ('qw', 4, 0, 1), ('mm', 4, 0, 0), ('mm', 4, 0, 1), ('silu', 4, 0), ('silu', 4, 1), ('qw', 4, 1, 0), ('cw2', 3, 'V'), ('qw', 4, 1, 1), ('mm', 4, 1, 0), ('mm', 4, 1, 1), ('qw2', 3), ('mmy', 3), ('h', 4, 0), ('h', 4, 1), ('cw2', 2, 'S'), ('cy', 3), ('qh', 4), ('qw2', 2), ('mmy', 2), ('cy', 2), ('cw2', 4, 'S'), ('qw2', 4), ('mmy', 4), ('cy', 4)]
+B = {"wraw":5,"w2raw":6,"wbf":4,"wq":12,"w2q":5,"w2bf":4,"xp1":2,"xp2":2,"xbf":3,"xq":10,"silu":4,"hq":5}
+
+
+def tile_moe_pre_glu_silu_kernel(tc, xT, w1, w3, w2, gate, offs, pos1, pos2, out):
+    nc = tc.nc
+
+    def cast(engine, dst, src):
+        if engine == "S":
+            nc.scalar.copy(out=dst, in_=src)
+        elif engine == "G":
+            nc.gpsimd.tensor_scalar(dst, src, 1.0, 0.0, MULT, ADD)
+        else:
+            nc.vector.tensor_copy(out=dst, in_=src)
+
+    def interleave(engine, rounded, src):
+        cast(
+            engine,
+            rounded.rearrange("p (c i j) -> p c j i", i=2, j=PACK),
+            src.rearrange("p j (c i) -> p c j i", i=2),
+        )
+
+    with ExitStack() as ctx:
+        keep = ctx.enter_context(tc.tile_pool(name="keep", bufs=1))
+        ring = ctx.enter_context(tc.tile_pool(name="ring", bufs=2))
+        psum = ctx.enter_context(tc.psum_pool(name="psum", bufs=1))
+
+        offs_sb = keep.tile([P, S // 16], U16, name="offs_sb")
+        pos1_sb = keep.tile([P, T // 16], U16, name="pos1_sb")
+        pos2_sb = keep.tile([P, T // 16], U16, name="pos2_sb")
+        gate_first = keep.tile([P, C], F32, name="gate_first")
+        gate_rest = keep.tile([P, S - C], F32, name="gate_rest")
+        tokens = [[keep.tile([P, T], F32, name=f"tokens{a}{j}") for j in range(PACK)] for a in range(PASSES)]
+        y_sb = keep.tile([P, N // P, S], F32, name="y_sb")
+        x_rows = xT.rearrange("(a p j) t -> a j p t", p=P, j=PACK)
+        t = {}
+
+        def quantize(tag, width, values):
+            codes = ring.tile([P, width], U32, name=tag + "_codes", bufs=B[tag], align_bytes=64)
+            scales = ring.tile([P, width], U8, name=tag + "_scales", bufs=B[tag], align_bytes=64)
+            nc.vector.quantize_mx(out=codes[:].bitcast(FP8X4), scales=scales[:], in_=values)
+            return codes, scales
+
+        warm_in = keep.tile([P, 1], F32, name="warm_in")
+        warm_out = keep.tile([P, 1], F32, name="warm_out")
+        nc.vector.memset(warm_in[:], 0.0)
+        nc.scalar.activation(out=warm_out[:], in_=warm_in[:], func=SILU)
+
+        for step in ORDER:
+            k = step[0]
+            r = tuple(step[1:])
+            if k == "lo":
+                nc.sync.dma_start(out=offs_sb[:], in_=offs)
+            elif k == "lp":
+                nc.sync.dma_start(out=pos1_sb[:], in_=pos1)
+                nc.sync.dma_start(out=pos2_sb[:], in_=pos2)
+            elif k == "lg":
+                if r[0] == 0:
+                    nc.sync.dma_start(out=gate_first[:], in_=gate[0:P, 0:C])
+                else:
+                    nc.sync.dma_start(out=gate_rest[:], in_=gate[0:P, C:S])
+            elif k == "lx":
+                nc.sync.dma_start(out=tokens[r[0]][r[1]][:], in_=x_rows[r[0], r[1]])
+            elif k == "lw":
+                e, m, a = r
+                t[("raw", e, m, a)] = ring.tile([P, PACK, H], F32, name="w_raw", bufs=B["wraw"])
+                src = (w1, w3)[m][e, a * K_PASS : (a + 1) * K_PASS, :]
+                nc.sync.dma_start(out=t[("raw", e, m, a)][:], in_=src.rearrange("(p j) c -> p j c", j=PACK))
+            elif k == "lw2":
+                e = r[0]
+                t[("raw2", e)] = ring.tile([P, PACK, N], F32, name="w2_raw", bufs=B["w2raw"])
+                nc.sync.dma_start(out=t[("raw2", e)][:], in_=w2[e].rearrange("(p j) c -> p j c", j=PACK))
+            elif k == "G":
+                e0, e1, a, j = r
+                if j == 0:
+                    picked = ring.tile([P, PACK, (e1 - e0) * C], F32, name=f"x_picked{e1 - e0}", bufs=B[f"xp{e1 - e0}"])
+                    t[("xg", e0, a)] = picked
+                    for e in range(e0, e1):
+                        t[("xp", e, a)] = picked[:, :, (e - e0) * C : (e - e0 + 1) * C]
+                g = gate_first[:] if e0 == 0 else gate_rest[:, (e0 - 1) * C : (e1 - 1) * C]
+                window = tokens[a][j][:].indirect(offs_sb[:, e0 * C // 16 : e1 * C // 16])
+                nc.vector.tensor_tensor(t[("xg", e0, a)][:, j, :], window, g, MULT)
+            elif k == "cx":
+                e, a, en = r
+                t[("xbf", e, a)] = ring.tile([P, PACK * C], BF16, name="x_bf", bufs=B["xbf"], align_bytes=64)
+                interleave(en, t[("xbf", e, a)][:], t[("xp", e, a)])
+            elif k == "qx":
+                t[("xq",) + r] = quantize("xq", C, t[("xbf",) + r][:])
+            elif k == "cw":
+                e, m, a, tp, en = r
+                if ("wbf", e, m, a) not in t:
+                    t[("wbf", e, m, a)] = ring.tile([P, PACK * H], BF16, name="w_bf", bufs=B["wbf"], align_bytes=64)
+                dst = t[("wbf", e, m, a)][:].rearrange("p (tp t2 q j) -> p tp q j t2", tp=2, t2=2, j=PACK)
+                src = t[("raw", e, m, a)][:].rearrange("p j (q tp t2) -> p tp q j t2", tp=2, t2=2)
+                if tp is None:
+                    cast(en, dst, src)
+                else:
+                    cast(en, dst[:, tp], src[:, tp])
+            elif k == "qw":
+                t[("wq",) + r] = quantize("wq", H, t[("wbf",) + r][:])
+            elif k == "cw2":
+                e, en = r
+                t[("w2bf", e)] = ring.tile([P, PACK * N], BF16, name="w2_bf", bufs=B["w2bf"], align_bytes=64)
+                interleave(en, t[("w2bf", e)][:], t[("raw2", e)][:])
+            elif k == "qw2":
+                t[("w2q",) + r] = quantize("w2q", N, t[("w2bf",) + r][:])
+            elif k == "mm":
+                e, m, half = r
+                bank = psum.tile([P, PACK, HALF], F32, name=f"bank{m}", bufs=3)
+                t[("b",) + r] = bank
+                slots = slice(half * HALF, (half + 1) * HALF)
+                for u in range(PACK):
+                    cols = slice(u * P, (u + 1) * P)
+                    for a in range(PASSES):
+                        wq = t[("wq", e, m, a)]
+                        xq = t[("xq", e, a)]
+                        nc.tensor.matmul_mx(
+                            out=bank[:, u, :],
+                            lhsT=wq[0][:, cols].bitcast(FP8X4),
+                            lhsT_scale=wq[1][:, cols],
+                            rhs=xq[0][:, slots].bitcast(FP8X4),
+                            rhs_scale=xq[1][:, slots],
+                            start=(a == 0),
+                            stop=(a == PASSES - 1),
+                        )
+            elif k == "silu":
+                e, half = r
+                t[("s",) + r] = ring.tile([P, HALF, PACK], F32, name="silu", bufs=B["silu"])
+                nc.scalar.activation(out=t[("s",) + r][:], in_=t[("b", e, 0, half)][:].rearrange("p u s -> p s u"), func=SILU)
+            elif k == "h":
+                e, half = r
+                if ("h", e) not in t:
+                    t[("h", e)] = ring.tile([P, C, PACK], BF16, name="h", bufs=2, align_bytes=64)
+                nc.vector.tensor_tensor(
+                    t[("h", e)][:, half * HALF : (half + 1) * HALF, :],
+                    t[("b", e, 1, half)][:].rearrange("p u s -> p s u"),
+                    t[("s", e, half)][:],
+                    MULT,
+                )
+            elif k == "qh":
+                t[("hq",) + r] = quantize("hq", C, t[("h",) + r][:].rearrange("p s u -> p (s u)"))
+            elif k == "mmy":
+                e = r[0]
+                bank = psum.tile([P, N // P, C], F32, name="bank_y", bufs=2)
+                t[("by", e)] = bank
+                for g in range(N // P):
+                    cols = slice(g * P, (g + 1) * P)
+                    nc.tensor.matmul_mx(
+                        out=bank[:, g, :],
+                        lhsT=t[("w2q", e)][0][:, cols].bitcast(FP8X4),
+                        lhsT_scale=t[("w2q", e)][1][:, cols],
+                        rhs=t[("hq", e)][0][:].bitcast(FP8X4),
+                        rhs_scale=t[("hq", e)][1][:],
+                        start=True,
+                        stop=True,
+                    )
+            elif k == "cy":
+                e = r[0]
+                nc.scalar.copy(out=y_sb[:, :, e * C : (e + 1) * C], in_=t[("by", e)][:])
+
+        for g in range(N // P):
+            first = ring.tile([P, T], F32, name="first", tag="w_raw", bufs=B["wraw"])
+            second = ring.tile([P, T], F32, name="second", tag="w_raw", bufs=B["wraw"])
+            total = ring.tile([P, T], F32, name="total", tag="w_raw", bufs=B["wraw"])
+            nc.vector.tensor_copy(first[:], y_sb[:, g, :].indirect(pos1_sb[:]))
+            nc.vector.tensor_copy(second[:], y_sb[:, g, :].indirect(pos2_sb[:]))
+            nc.vector.tensor_tensor(total[:], first[:], second[:], ADD)
+            nc.sync.dma_start(out=out[g * P : (g + 1) * P, :], in_=total[:])

@@ -23,8 +23,8 @@ MULT = mybir.AluOpType.mult
 ADD = mybir.AluOpType.add
 SILU = mybir.ActivationFunctionType.Silu
 
-ORDER = [('lo',), ('lg', 0), ('lx', 0, 0), ('lx', 0, 1), ('lg', 1), ('lw', 0, 0, 0), ('lx', 0, 2), ('lw', 0, 0, 1), ('lw', 0, 1, 0), ('lx', 0, 3), ('lw', 0, 1, 1), ('lx', 1, 0), ('lw', 1, 0, 0), ('lx', 1, 1), ('lx', 1, 2), ('lw', 1, 0, 1), ('lw', 1, 1, 0), ('lw', 1, 1, 1), ('lx', 1, 3), ('lw', 2, 0, 0), ('lw', 2, 0, 1), ('lw', 2, 1, 0), ('lw', 2, 1, 1), ('lw', 3, 0, 0), ('lw', 3, 0, 1), ('lw', 3, 1, 0), ('lw', 3, 1, 1), ('lw', 4, 0, 0), ('lw', 4, 0, 1), ('lw', 4, 1, 0), ('lw', 4, 1, 1), ('lw2', 0), ('lw2', 1), ('lw2', 2), ('lw2', 3), ('lp',), ('lw2', 4), ('G', 0, 1, 0, 0), ('G', 1, 3, 0, 0), ('G', 0, 1, 0, 1), ('G', 1, 3, 0, 1), ('G', 0, 1, 0, 2), ('cw', 0, 0, 0, None, 'S'), ('G', 1, 3, 0, 2), ('G', 3, 5, 0, 0), ('G', 0, 1, 0, 3), ('cw', 0, 0, 1, None, 'S'), ('G', 1, 3, 0, 3), ('G', 3, 5, 0, 1), ('G', 0, 1, 1, 0), ('cw', 0, 1, 0, None, 'S'), ('G', 1, 3, 1, 0), ('qw', 0, 0, 0), ('G', 3, 5, 0, 2), ('cw', 0, 1, 1, None, 'S'), ('G', 0, 1, 1, 1), ('G', 1, 3, 1, 1), ('qw', 0, 0, 1), ('G', 3, 5, 0, 3), ('cw', 1, 0, 0, None, 'S'), ('G', 0, 1, 1, 2), ('G', 1, 3, 1, 2), ('qw', 0, 1, 0), ('cw', 1, 0, 1, None, 'S'), ('G', 3, 5, 1, 0), ('G', 0, 1, 1, 3), ('G', 1, 3, 1, 3), ('qw', 0, 1, 1), ('cw', 1, 1, 0, None, 'S'), ('G', 3, 5, 1, 1), ('qw', 1, 0, 0), ('cx', 0, 0, 'S'), ('cw', 1, 1, 1, None, 'S'), ('G', 3, 5, 1, 2), ('cx', 1, 0, 'V'), ('qw', 1, 0, 1), ('cx', 0, 1, 'S'), ('qx', 0, 0), ('cw', 2, 0, 0, 0, 'S'), ('cw', 2, 0, 0, 1, 'V'), ('cx', 2, 0, 'S'), ('G', 3, 5, 1, 3), ('cw2', 0, 'V'), ('qx', 1, 0), ('qw', 1, 1, 0), ('qx', 0, 1), ('mm', 0, 0, 0), ('mm', 0, 0, 1), ('mm', 0, 1, 0), ('mm', 0, 1, 1), ('cx', 1, 1, 'S'), ('cx', 3, 0, 'S'), ('qw2', 0), ('cw', 2, 0, 1, None, 'S'), ('qx', 2, 0), ('silu', 0, 0), ('silu', 0, 1), ('cx', 4, 0, 'S'), ('qw', 1, 1, 1), ('qx', 1, 1), ('h', 0, 0), ('h', 0, 1), ('mm', 1, 0, 0), ('mm', 1, 0, 1), ('mm', 1, 1, 0), ('mm', 1, 1, 1), ('qx', 3, 0), ('cx', 2, 1, 'S'), ('cw', 2, 1, 0, None, 'V'), ('qh', 0), ('mmy', 0), ('silu', 1, 0), ('silu', 1, 1), ('qw', 2, 0, 0), ('qx', 4, 0), ('cy', 0), ('qx', 2, 1), ('h', 1, 0), ('h', 1, 1), ('cw', 2, 1, 1, 0, 'S'), ('cw', 2, 1, 1, 1, 'V'), ('cx', 3, 1, 'V'), ('qh', 1), ('qw', 2, 0, 1), ('mm', 2, 0, 0), ('mm', 2, 0, 1), ('cw', 3, 0, 0, 0, 'S'), ('cw', 3, 0, 0, 1, 'V'), ('silu', 2, 0), ('silu', 2, 1), ('qx', 3, 1), ('cx', 4, 1, 'S'), ('qw', 2, 1, 0), ('cw', 3, 0, 1, 0, 'S'), ('cw', 3, 0, 1, 1, 'V'), ('qx', 4, 1), ('qw', 2, 1, 1), ('mm', 2, 1, 0), ('mm', 2, 1, 1), ('cw', 3, 1, 0, 0, 'S'), ('cw', 3, 1, 0, 1, 'V'), ('h', 2, 0), ('h', 2, 1), ('qw', 3, 0, 0), ('qh', 2), ('cw', 3, 1, 1, None, 'S'), ('qw', 3, 0, 1), ('mm', 3, 0, 0), ('mm', 3, 0, 1), ('cw', 4, 0, 0, 0, 'S'), ('cw', 4, 0, 0, 1, 'V'), ('cw2', 1, 'V'), ('silu', 3, 0), ('silu', 3, 1), ('qw', 3, 1, 0), ('qw2', 1), ('mmy', 1), ('cw', 4, 0, 1, None, 'V'), ('cy', 1), ('qw', 3, 1, 1), ('mm', 3, 1, 0), ('mm', 3, 1, 1), ('cw', 4, 1, 0, None, 'S'), ('h', 3, 0), ('h', 3, 1), ('qw', 4, 0, 0), ('qh', 3), ('cw', 4, 1, 1, None, 'V'), ('qw', 4, 0, 1), ('mm', 4, 0, 0), ('mm', 4, 0, 1), ('silu', 4, 0), ('silu', 4, 1), ('qw', 4, 1, 0), ('cw2', 3, 'V'), ('qw', 4, 1, 1), ('mm', 4, 1, 0), ('mm', 4, 1, 1), ('qw2', 3), ('mmy', 3), ('h', 4, 0), ('h', 4, 1), ('cw2', 2, 'S'), ('cy', 3), ('qh', 4), ('qw2', 2), ('mmy', 2), ('cy', 2), ('cw2', 4, 'S'), ('qw2', 4), ('mmy', 4), ('cy', 4)]
-B = {"wraw":5,"w2raw":6,"wbf":4,"wq":12,"w2q":5,"w2bf":4,"xp1":2,"xp2":2,"xbf":3,"xq":10,"silu":4,"hq":5}
+ORDER = [('lg', 0), ('lo',), ('lx', 0, 0), ('lx', 0, 1), ('lg', 1), ('lw', 0, 0, 0), ('lx', 0, 2), ('lp',), ('lw', 0, 0, 1), ('lw', 0, 1, 0), ('lx', 0, 3), ('lw', 0, 1, 1), ('lx', 1, 0), ('lx', 1, 1), ('lw', 1, 0, 0), ('lw', 1, 0, 1), ('lx', 1, 2), ('lw', 1, 1, 0), ('lw', 1, 1, 1), ('lx', 1, 3), ('lw', 2, 0, 0), ('lw', 2, 0, 1), ('lw', 2, 1, 0), ('lw', 2, 1, 1), ('lw', 3, 0, 0), ('lw', 3, 0, 1), ('lw', 3, 1, 0), ('lw', 3, 1, 1), ('lw', 4, 0, 0), ('lw', 4, 0, 1), ('lw', 4, 1, 0), ('lw', 4, 1, 1), ('lw2', 0), ('lw2', 1), ('lw2', 2), ('lw2', 3), ('lw2', 4), ('G', 0, 1, 0, 0, 'c'), ('G', 0, 1, 0, 1, 'c'), ('cw', 0, 0, 0, None, 'S'), ('G', 0, 1, 0, 2, 'c'), ('G', 1, 3, 0, 0, 'c'), ('cw2', 0, 'V'), ('qw2', 0), ('G', 0, 1, 0, 3, 'c'), ('cw', 0, 0, 1, None, 'S'), ('G', 1, 3, 0, 1, 'c'), ('G', 1, 3, 0, 2, 'c'), ('cw', 0, 1, 0, None, 'S'), ('G', 1, 3, 0, 3, 'c'), ('cw', 0, 1, 1, None, 'S'), ('G', 0, 1, 1, 0, 'c'), ('cx', 0, 0, 'S'), ('G', 0, 1, 1, 1, 'c'), ('cw', 1, 0, 0, 0, 'S'), ('cw', 1, 0, 0, 1, 'V'), ('G', 0, 1, 1, 2, 'c'), ('G', 3, 5, 1, 0, 'c'), ('cw', 1, 0, 1, None, 'S'), ('cx', 1, 0, 'S'), ('cx', 2, 0, 'S'), ('G', 3, 5, 0, 0, 'c'), ('G', 0, 1, 1, 3, 'c'), ('G', 3, 5, 1, 1, 'c'), ('G', 1, 3, 1, 0, 'c'), ('cw', 1, 1, 0, None, 'S'), ('G', 3, 5, 0, 1, 'c'), ('G', 3, 5, 1, 2, 'c'), ('G', 1, 3, 1, 1, 'c'), ('G', 3, 5, 0, 2, 'c'), ('cw', 1, 1, 1, None, 'S'), ('G', 3, 5, 1, 3, 'c'), ('G', 1, 3, 1, 2, 'c'), ('G', 3, 5, 0, 3, 'c'), ('cx', 0, 1, 'S'), ('cw', 2, 0, 0, 0, 'S'), ('cw', 2, 0, 0, 1, 'V'), ('G', 1, 3, 1, 3, 'c'), ('qw', 0, 0, None), ('cw', 2, 0, 1, None, 'S'), ('cx', 3, 1, 'S'), ('cx', 4, 1, 'V'), ('cw', 2, 1, 0, None, 'V'), ('cx', 3, 0, 'S'), ('cx', 4, 0, 'V'), ('cx', 1, 1, 'S'), ('cx', 2, 1, 'S'), ('qw', 0, 1, None), ('cw', 2, 1, 1, None, 'S'), ('qx', 0, None), ('mm', 0, 0, 0), ('mm', 0, 0, 1), ('mm', 0, 1, 0), ('mm', 0, 1, 1), ('cw', 3, 0, 0, None, 'V'), ('qx', 4, 1), ('qw', 1, 0, None), ('cw', 3, 0, 1, None, 'S'), ('qx', 3, None), ('qx', 4, 0), ('qx', 1, None), ('qx', 2, None), ('mm', 1, 0, 0), ('mm', 1, 0, 1), ('cw', 3, 1, 0, None, 'S'), ('qw', 1, 1, None), ('mm', 1, 1, 0), ('mm', 1, 1, 1), ('cw', 3, 1, 1, None, 'V'), ('silu', 0, 0), ('silu', 0, 1), ('h', 0, 0), ('h', 0, 1), ('cw2', 1, 'S'), ('qh', 0), ('mmy', 0), ('cw', 4, 0, 0, 0, 'S'), ('cw', 4, 0, 0, 1, 'V'), ('qw2', 1), ('cy', 0), ('qw', 2, 0, None), ('mm', 2, 0, 0), ('mm', 2, 0, 1), ('cw', 4, 0, 1, None, 'S'), ('qw', 2, 1, 0), ('cw', 4, 1, 0, None, 'S'), ('silu', 1, 0), ('silu', 1, 1), ('h', 1, 0), ('h', 1, 1), ('qh', 1), ('mmy', 1), ('qw', 2, 1, 1), ('mm', 2, 1, 0), ('mm', 2, 1, 1), ('cw', 4, 1, 1, None, 'V'), ('cy', 1), ('cw2', 4, 'S'), ('qw', 3, 0, 0), ('qw2', 4), ('qw', 3, 0, 1), ('mm', 3, 0, 0), ('mm', 3, 0, 1), ('silu', 2, 0), ('silu', 2, 1), ('h', 2, 0), ('h', 2, 1), ('qh', 2), ('qw', 3, 1, None), ('mm', 3, 1, 0), ('mm', 3, 1, 1), ('qw', 4, 0, 0), ('qw', 4, 0, 1), ('mm', 4, 0, 0), ('mm', 4, 0, 1), ('silu', 3, 0), ('silu', 3, 1), ('h', 3, 0), ('h', 3, 1), ('qh', 3), ('qw', 4, 1, None), ('mm', 4, 1, 0), ('mm', 4, 1, 1), ('cw2', 2, 'S'), ('cw2', 3, 'V'), ('qw2', 2), ('mmy', 2), ('qw2', 3), ('mmy', 3), ('silu', 4, 0), ('silu', 4, 1), ('h', 4, 0), ('h', 4, 1), ('cy', 2), ('cy', 3), ('qh', 4), ('mmy', 4), ('cy', 4), ('tail', 0, 0, 640, 'G'), ('tail', 1, 0, 320, 'G'), ('tail', 1, 320, 640, 'V')]
+B = {"wraw":7,"wbf":2,"wq":4,"w2q":2,"w2bf":4,"xp1":2,"xp2":3,"xbf":4,"xq":7,"silu":7,"hq":3}
 
 
 def tile_moe_pre_glu_silu_kernel(tc, xT, w1, w3, w2, gate, offs, pos1, pos2, out):
@@ -60,6 +60,23 @@ def tile_moe_pre_glu_silu_kernel(tc, xT, w1, w3, w2, gate, offs, pos1, pos2, out
         x_rows = xT.rearrange("(a p j) t -> a j p t", p=P, j=PACK)
         t = {}
 
+        def gate_cols(lo, hi):
+            return gate_first[:, lo:hi] if lo < C else gate_rest[:, lo - C : hi - C]
+
+        def quantize2(key, tag, width, values, a):
+            if key not in t:
+                codes = ring.tile([P, PASSES, width], U32, name=tag + "_codes", bufs=B[tag], align_bytes=64)
+                scales = ring.tile([P, PASSES, width], U8, name=tag + "_scales", bufs=B[tag], align_bytes=64)
+                t[key] = (codes, scales)
+            codes, scales = t[key]
+            if a is None:
+                flat = "p a c -> p (a c)"
+                nc.vector.quantize_mx(
+                    out=codes[:].rearrange(flat).bitcast(FP8X4), scales=scales[:].rearrange(flat), in_=values[:].rearrange(flat)
+                )
+            else:
+                nc.vector.quantize_mx(out=codes[:, a, :].bitcast(FP8X4), scales=scales[:, a, :], in_=values[:, a, :])
+
         def quantize(tag, width, values):
             codes = ring.tile([P, width], U32, name=tag + "_codes", bufs=B[tag], align_bytes=64)
             scales = ring.tile([P, width], U8, name=tag + "_scales", bufs=B[tag], align_bytes=64)
@@ -93,36 +110,51 @@ def tile_moe_pre_glu_silu_kernel(tc, xT, w1, w3, w2, gate, offs, pos1, pos2, out
                 nc.sync.dma_start(out=t[("raw", e, m, a)][:], in_=src.rearrange("(p j) c -> p j c", j=PACK))
             elif k == "lw2":
                 e = r[0]
-                t[("raw2", e)] = ring.tile([P, PACK, N], F32, name="w2_raw", bufs=B["w2raw"])
+                t[("raw2", e)] = ring.tile([P, PACK, N], F32, name="w2_raw", tag="w_raw", bufs=B["wraw"])
                 nc.sync.dma_start(out=t[("raw2", e)][:], in_=w2[e].rearrange("(p j) c -> p j c", j=PACK))
             elif k == "G":
-                e0, e1, a, j = r
+                e0, e1, a, j, md = r
                 if j == 0:
                     picked = ring.tile([P, PACK, (e1 - e0) * C], F32, name=f"x_picked{e1 - e0}", bufs=B[f"xp{e1 - e0}"])
                     t[("xg", e0, a)] = picked
                     for e in range(e0, e1):
                         t[("xp", e, a)] = picked[:, :, (e - e0) * C : (e - e0 + 1) * C]
-                g = gate_first[:] if e0 == 0 else gate_rest[:, (e0 - 1) * C : (e1 - 1) * C]
                 window = tokens[a][j][:].indirect(offs_sb[:, e0 * C // 16 : e1 * C // 16])
-                nc.vector.tensor_tensor(t[("xg", e0, a)][:, j, :], window, g, MULT)
+                if md == "c":
+                    nc.vector.tensor_tensor(t[("xg", e0, a)][:, j, :], window, gate_cols(e0 * C, e1 * C), MULT)
+                else:
+                    nc.vector.tensor_copy(t[("xg", e0, a)][:, j, :], window)
             elif k == "cx":
                 e, a, en = r
-                t[("xbf", e, a)] = ring.tile([P, PACK * C], BF16, name="x_bf", bufs=B["xbf"], align_bytes=64)
-                interleave(en, t[("xbf", e, a)][:], t[("xp", e, a)])
+                if ("xbf", e) not in t:
+                    t[("xbf", e)] = ring.tile([P, PASSES, PACK * C], BF16, name="x_bf", bufs=B["xbf"], align_bytes=64)
+                if en == "G":
+                    for half in range(2):
+                        lo, hi = half * HALF, (half + 1) * HALF
+                        nc.gpsimd.tensor_tensor(
+                            t[("xbf", e)][:, a, PACK * lo : PACK * hi].rearrange("p (s j) -> p s j", j=PACK),
+                            t[("xp", e, a)][:, :, lo:hi].rearrange("p j s -> p s j"),
+                            gate_cols(e * C + lo, e * C + hi).unsqueeze(2).to_broadcast([P, HALF, PACK]),
+                            MULT,
+                        )
+                else:
+                    interleave(en, t[("xbf", e)][:, a, :], t[("xp", e, a)])
             elif k == "qx":
-                t[("xq",) + r] = quantize("xq", C, t[("xbf",) + r][:])
+                e, a = r
+                quantize2(("xq", e), "xq", C, t[("xbf", e)], a)
             elif k == "cw":
                 e, m, a, tp, en = r
-                if ("wbf", e, m, a) not in t:
-                    t[("wbf", e, m, a)] = ring.tile([P, PACK * H], BF16, name="w_bf", bufs=B["wbf"], align_bytes=64)
-                dst = t[("wbf", e, m, a)][:].rearrange("p (tp t2 q j) -> p tp q j t2", tp=2, t2=2, j=PACK)
+                if ("wbf", e, m) not in t:
+                    t[("wbf", e, m)] = ring.tile([P, PASSES, PACK * H], BF16, name="w_bf", bufs=B["wbf"], align_bytes=64)
+                dst = t[("wbf", e, m)][:, a, :].rearrange("p (tp t2 q j) -> p tp q j t2", tp=2, t2=2, j=PACK)
                 src = t[("raw", e, m, a)][:].rearrange("p j (q tp t2) -> p tp q j t2", tp=2, t2=2)
                 if tp is None:
                     cast(en, dst, src)
                 else:
                     cast(en, dst[:, tp], src[:, tp])
             elif k == "qw":
-                t[("wq",) + r] = quantize("wq", H, t[("wbf",) + r][:])
+                e, m, a = r
+                quantize2(("wq", e, m), "wq", H, t[("wbf", e, m)], a)
             elif k == "cw2":
                 e, en = r
                 t[("w2bf", e)] = ring.tile([P, PACK * N], BF16, name="w2_bf", bufs=B["w2bf"], align_bytes=64)
@@ -137,14 +169,14 @@ def tile_moe_pre_glu_silu_kernel(tc, xT, w1, w3, w2, gate, offs, pos1, pos2, out
                 for u in range(PACK):
                     cols = slice(u * P, (u + 1) * P)
                     for a in range(PASSES):
-                        wq = t[("wq", e, m, a)]
-                        xq = t[("xq", e, a)]
+                        wq = t[("wq", e, m)]
+                        xq = t[("xq", e)]
                         nc.tensor.matmul_mx(
                             out=bank[:, u, :],
-                            lhsT=wq[0][:, cols].bitcast(FP8X4),
-                            lhsT_scale=wq[1][:, cols],
-                            rhs=xq[0][:, slots].bitcast(FP8X4),
-                            rhs_scale=xq[1][:, slots],
+                            lhsT=wq[0][:, a, cols].bitcast(FP8X4),
+                            lhsT_scale=wq[1][:, a, cols],
+                            rhs=xq[0][:, a, slots].bitcast(FP8X4),
+                            rhs_scale=xq[1][:, a, slots],
                             start=(a == 0),
                             stop=(a == PASSES - 1),
                         )
@@ -181,13 +213,18 @@ def tile_moe_pre_glu_silu_kernel(tc, xT, w1, w3, w2, gate, offs, pos1, pos2, out
                     )
             elif k == "cy":
                 e = r[0]
-                nc.scalar.copy(out=y_sb[:, :, e * C : (e + 1) * C], in_=t[("by", e)][:])
-
-        for g in range(N // P):
-            first = ring.tile([P, T], F32, name="first", tag="w_raw", bufs=B["wraw"])
-            second = ring.tile([P, T], F32, name="second", tag="w_raw", bufs=B["wraw"])
-            total = ring.tile([P, T], F32, name="total", tag="w_raw", bufs=B["wraw"])
-            nc.vector.tensor_copy(first[:], y_sb[:, g, :].indirect(pos1_sb[:]))
-            nc.vector.tensor_copy(second[:], y_sb[:, g, :].indirect(pos2_sb[:]))
-            nc.vector.tensor_tensor(total[:], first[:], second[:], ADD)
-            nc.sync.dma_start(out=out[g * P : (g + 1) * P, :], in_=total[:])
+                if e + 1 < E:
+                    nc.scalar.copy(out=y_sb[:, :, e * C : (e + 1) * C], in_=t[("by", e)][:])
+                else:
+                    for g in range(N // P):
+                        nc.scalar.copy(out=y_sb[:, g, e * C : (e + 1) * C], in_=t[("by", e)][:, g, :])
+            elif k == "tail":
+                g, lo, hi, en = r
+                first = ring.tile([P, hi - lo], F32, name="first", tag="w_raw", bufs=B["wraw"])
+                second = ring.tile([P, hi - lo], F32, name="second", tag="w_raw", bufs=B["wraw"])
+                total = ring.tile([P, hi - lo], F32, name="total", tag="w_raw", bufs=B["wraw"])
+                cols = slice(lo // 16, hi // 16)
+                nc.vector.tensor_copy(first[:], y_sb[:, g, :].indirect(pos1_sb[:, cols]))
+                nc.vector.tensor_copy(second[:], y_sb[:, g, :].indirect(pos2_sb[:, cols]))
+                (nc.vector if en == "V" else nc.gpsimd).tensor_tensor(total[:], first[:], second[:], ADD)
+                nc.sync.dma_start(out=out[g * P : (g + 1) * P, lo:hi], in_=total[:])

@@ -23,8 +23,10 @@ MULT = mybir.AluOpType.mult
 ADD = mybir.AluOpType.add
 SILU = mybir.ActivationFunctionType.Silu
 
-ORDER = [('lg', 0), ('lo',), ('lx', 0, 0), ('lx', 0, 1), ('lg', 1), ('lw', 0, 0, 0), ('lx', 0, 2), ('lp',), ('lw', 0, 0, 1), ('lw', 0, 1, 0), ('lx', 0, 3), ('lw', 0, 1, 1), ('lx', 1, 0), ('lx', 1, 1), ('lw', 1, 0, 0), ('lw', 1, 0, 1), ('lx', 1, 2), ('lw', 1, 1, 0), ('lw', 1, 1, 1), ('lx', 1, 3), ('lw', 2, 0, 0), ('lw', 2, 0, 1), ('lw', 2, 1, 0), ('lw', 2, 1, 1), ('lw', 3, 0, 0), ('lw', 3, 0, 1), ('lw', 3, 1, 0), ('lw', 3, 1, 1), ('lw', 4, 0, 0), ('lw', 4, 0, 1), ('lw', 4, 1, 0), ('lw', 4, 1, 1), ('lw2', 0), ('lw2', 1), ('lw2', 2), ('lw2', 3), ('lw2', 4), ('G', 0, 1, 0, 0, 'c'), ('G', 0, 1, 0, 1, 'c'), ('cw', 0, 0, 0, None, 'S'), ('G', 0, 1, 0, 2, 'c'), ('G', 1, 3, 0, 0, 'c'), ('cw2', 0, 'V'), ('qw2', 0), ('G', 0, 1, 0, 3, 'c'), ('cw', 0, 0, 1, None, 'S'), ('G', 1, 3, 0, 1, 'c'), ('G', 1, 3, 0, 2, 'c'), ('cw', 0, 1, 0, None, 'S'), ('G', 1, 3, 0, 3, 'c'), ('cw', 0, 1, 1, None, 'S'), ('G', 0, 1, 1, 0, 'c'), ('cx', 0, 0, 'S'), ('G', 0, 1, 1, 1, 'c'), ('cw', 1, 0, 0, 0, 'S'), ('cw', 1, 0, 0, 1, 'V'), ('G', 0, 1, 1, 2, 'c'), ('G', 3, 5, 1, 0, 'c'), ('cw', 1, 0, 1, None, 'S'), ('cx', 1, 0, 'S'), ('cx', 2, 0, 'S'), ('G', 3, 5, 0, 0, 'c'), ('G', 0, 1, 1, 3, 'c'), ('G', 3, 5, 1, 1, 'c'), ('G', 1, 3, 1, 0, 'c'), ('cw', 1, 1, 0, None, 'S'), ('G', 3, 5, 0, 1, 'c'), ('G', 3, 5, 1, 2, 'c'), ('G', 1, 3, 1, 1, 'c'), ('G', 3, 5, 0, 2, 'c'), ('cw', 1, 1, 1, None, 'S'), ('G', 3, 5, 1, 3, 'c'), ('G', 1, 3, 1, 2, 'c'), ('G', 3, 5, 0, 3, 'c'), ('cx', 0, 1, 'S'), ('cw', 2, 0, 0, 0, 'S'), ('cw', 2, 0, 0, 1, 'V'), ('G', 1, 3, 1, 3, 'c'), ('qw', 0, 0, None), ('cw', 2, 0, 1, None, 'S'), ('cx', 3, 1, 'S'), ('cx', 4, 1, 'V'), ('cw', 2, 1, 0, None, 'V'), ('cx', 3, 0, 'S'), ('cx', 4, 0, 'V'), ('cx', 1, 1, 'S'), ('cx', 2, 1, 'S'), ('qw', 0, 1, None), ('cw', 2, 1, 1, None, 'S'), ('qx', 0, None), ('mm', 0, 0, 0), ('mm', 0, 0, 1), ('mm', 0, 1, 0), ('mm', 0, 1, 1), ('cw', 3, 0, 0, None, 'V'), ('qx', 4, 1), ('qw', 1, 0, None), ('cw', 3, 0, 1, None, 'S'), ('qx', 3, None), ('qx', 4, 0), ('qx', 1, None), ('qx', 2, None), ('mm', 1, 0, 0), ('mm', 1, 0, 1), ('cw', 3, 1, 0, None, 'S'), ('qw', 1, 1, None), ('mm', 1, 1, 0), ('mm', 1, 1, 1), ('cw', 3, 1, 1, None, 'V'), ('silu', 0, 0), ('silu', 0, 1), ('h', 0, 0), ('h', 0, 1), ('cw2', 1, 'S'), ('qh', 0), ('mmy', 0), ('cw', 4, 0, 0, 0, 'S'), ('cw', 4, 0, 0, 1, 'V'), ('qw2', 1), ('cy', 0), ('qw', 2, 0, None), ('mm', 2, 0, 0), ('mm', 2, 0, 1), ('cw', 4, 0, 1, None, 'S'), ('qw', 2, 1, 0), ('cw', 4, 1, 0, None, 'S'), ('silu', 1, 0), ('silu', 1, 1), ('h', 1, 0), ('h', 1, 1), ('qh', 1), ('mmy', 1), ('qw', 2, 1, 1), ('mm', 2, 1, 0), ('mm', 2, 1, 1), ('cw', 4, 1, 1, None, 'V'), ('cy', 1), ('cw2', 4, 'S'), ('qw', 3, 0, 0), ('qw2', 4), ('qw', 3, 0, 1), ('mm', 3, 0, 0), ('mm', 3, 0, 1), ('silu', 2, 0), ('silu', 2, 1), ('h', 2, 0), ('h', 2, 1), ('qh', 2), ('qw', 3, 1, None), ('mm', 3, 1, 0), ('mm', 3, 1, 1), ('qw', 4, 0, 0), ('qw', 4, 0, 1), ('mm', 4, 0, 0), ('mm', 4, 0, 1), ('silu', 3, 0), ('silu', 3, 1), ('h', 3, 0), ('h', 3, 1), ('qh', 3), ('qw', 4, 1, None), ('mm', 4, 1, 0), ('mm', 4, 1, 1), ('cw2', 2, 'S'), ('cw2', 3, 'V'), ('qw2', 2), ('mmy', 2), ('qw2', 3), ('mmy', 3), ('silu', 4, 0), ('silu', 4, 1), ('h', 4, 0), ('h', 4, 1), ('cy', 2), ('cy', 3), ('qh', 4), ('mmy', 4), ('cy', 4), ('tail', 0, 0, 640, 'G'), ('tail', 1, 0, 320, 'G'), ('tail', 1, 320, 640, 'V')]
-B = {"wraw":7,"wbf":2,"wq":4,"w2q":2,"w2bf":4,"xp1":2,"xp2":3,"xbf":4,"xq":7,"silu":7,"hq":3}
+ORDER = [('lx', 0, 0), ('lo',), ('lg', 0), ('lx', 0, 1), ('lg', 1), ('lx', 0, 2), ('lw', 0, 0, 0), ('lw', 0, 0, 1), ('lw', 0, 1, 0), ('lx', 0, 3), ('lx', 1, 0), ('lx', 1, 1), ('lw', 0, 1, 1), ('lw', 1, 0, 0), ('lx', 1, 2), ('lw', 1, 0, 1), ('lw', 1, 1, 0), ('lw', 1, 1, 1), ('lw', 2, 0, 0), ('lw', 2, 0, 1), ('lw', 2, 1, 0), ('lx', 1, 3), ('lw', 2, 1, 1), ('lw', 3, 0, 0), ('lw', 3, 0, 1), ('lw', 3, 1, 0), ('lp',), ('lw', 3, 1, 1), ('lw', 4, 0, 0), ('lw', 4, 0, 1), ('lw', 4, 1, 0), ('lw2', 0, 2), ('lw', 4, 1, 1), ('lw2', 2, 4), ('lw2', 4, 5), ('G', 0, 2, 0, 0, 'c'), ('G', 0, 2, 0, 1, 'c'), ('G', 0, 2, 0, 2, 'c'), ('G', 0, 2, 0, 3, 'c'), ('G', 2, 6, 0, 0, 'c'), ('G', 2, 6, 0, 1, 'c'), ('G', 2, 6, 0, 2, 'c'), ('G', 2, 6, 0, 3, 'c'), ('cx', 0, 2, 0, 'S'), ('cx', 2, 6, 0, 'S'), ('G', 0, 2, 1, 0, 'c'), ('G', 0, 2, 1, 1, 'c'), ('G', 0, 2, 1, 2, 'c'), ('G', 0, 2, 1, 3, 'c'), ('G', 6, 10, 0, 0, 'c'), ('G', 6, 10, 0, 1, 'c'), ('G', 6, 10, 0, 2, 'c'), ('G', 6, 10, 0, 3, 'c'), ('cx', 0, 2, 1, 'V'), ('cx', 6, 10, 0, 'S'), ('G', 2, 6, 1, 0, 'c'), ('G', 2, 6, 1, 1, 'c'), ('G', 2, 6, 1, 2, 'c'), ('G', 2, 6, 1, 3, 'c'), ('cx', 2, 6, 1, 'V'), ('G', 6, 10, 1, 0, 'c'), ('G', 6, 10, 1, 1, 'c'), ('G', 6, 10, 1, 2, 'c'), ('G', 6, 10, 1, 3, 'c'), ('cx', 6, 10, 1, 'S'), ('qx', 0, 2, 0), ('cw2', 0, 2, 'V'), ('qw2', 0, 2), ('qx', 0, 2, 1), ('cw', 0, 0, 0, None, 'S'), ('cw', 0, 0, 1, None, 'S'), ('qx', 2, 10, 0), ('cw', 0, 1, 0, None, 'S'), ('cw', 0, 1, 1, None, 'S'), ('cw', 1, 0, 0, None, 'S'), ('qw', 0, 0, None), ('mm', 0, 0, 0), ('mm', 0, 0, 1), ('cw', 1, 0, 1, None, 'S'), ('qx', 2, 6, 1), ('cw', 1, 1, 0, None, 'S'), ('qw', 0, 1, None), ('mm', 0, 1, 0), ('mm', 0, 1, 1), ('cw', 1, 1, 1, None, 'V'), ('cw', 2, 0, 0, None, 'S'), ('qw', 1, 0, None), ('mm', 1, 0, 0), ('mm', 1, 0, 1), ('cw', 2, 0, 1, None, 'S'), ('qx', 6, 10, 1), ('cw', 2, 1, 0, None, 'S'), ('qw', 1, 1, None), ('mm', 1, 1, 0), ('mm', 1, 1, 1), ('cw', 2, 1, 1, 0, 'S'), ('cw', 2, 1, 1, 1, 'V'), ('cw', 3, 0, 0, None, 'V'), ('silu', 0, 0), ('silu', 0, 1), ('h', 0, 0), ('h', 0, 1), ('qw', 2, 0, None), ('mm', 2, 0, 0), ('mm', 2, 0, 1), ('qh', 0), ('mmy', 0), ('cw', 3, 0, 1, None, 'S'), ('cy', 0), ('cw', 3, 1, 0, None, 'S'), ('qw', 2, 1, None), ('mm', 2, 1, 0), ('mm', 2, 1, 1), ('cw', 3, 1, 1, None, 'V'), ('cw', 4, 0, 0, 0, 'S'), ('cw', 4, 0, 0, 1, 'V'), ('silu', 1, 0), ('silu', 1, 1), ('h', 1, 0), ('h', 1, 1), ('qw', 3, 0, None), ('mm', 3, 0, 0), ('mm', 3, 0, 1), ('qh', 1), ('mmy', 1), ('cw', 4, 0, 1, None, 'S'), ('cy', 1), ('cw', 4, 1, 0, None, 'S'), ('qw', 3, 1, None), ('mm', 3, 1, 0), ('mm', 3, 1, 1), ('cw', 4, 1, 1, None, 'V'), ('silu', 2, 0), ('silu', 2, 1), ('h', 2, 0), ('h', 2, 1), ('qw', 4, 0, None), ('mm', 4, 0, 0), ('mm', 4, 0, 1), ('qh', 2), ('qw', 4, 1, None), ('mm', 4, 1, 0), ('mm', 4, 1, 1), ('silu', 3, 0), ('silu', 3, 1), ('h', 3, 0), ('h', 3, 1), ('qh', 3), ('cw2', 2, 4, 'S'), ('qw2', 2, 4), ('mmy', 2), ('mmy', 3), ('cy', 2), ('cy', 3), ('silu', 4, 0), ('silu', 4, 1), ('h', 4, 0), ('h', 4, 1), ('qh', 4), ('cw2', 4, 5, 'V'), ('qw2', 4, 5), ('mmy', 4), ('cy', 4), ('tail', 0, 0, 640, 'G'), ('tail', 1, 0, 320, 'G'), ('tail', 1, 320, 640, 'V')]
+B = {"wraw":7,"wbf":4,"wq":4,"w2q":3,"w2bf":2,"xp2":1,"xp4":2,"silu":5,"hq":2,"gs":2}
+GS = B["gs"] * HALF
+TW = T + 0
 
 
 def tile_moe_pre_glu_silu_kernel(tc, xT, w1, w3, w2, gate, offs, pos1, pos2, out):
@@ -41,8 +43,8 @@ def tile_moe_pre_glu_silu_kernel(tc, xT, w1, w3, w2, gate, offs, pos1, pos2, out
     def interleave(engine, rounded, src):
         cast(
             engine,
-            rounded.rearrange("p (c i j) -> p c j i", i=2, j=PACK),
-            src.rearrange("p j (c i) -> p c j i", i=2),
+            rounded.rearrange("p (c i j) -> p c j i", i=4, j=PACK),
+            src.rearrange("p j (c i) -> p c j i", i=4),
         )
 
     with ExitStack() as ctx:
@@ -53,15 +55,18 @@ def tile_moe_pre_glu_silu_kernel(tc, xT, w1, w3, w2, gate, offs, pos1, pos2, out
         offs_sb = keep.tile([P, S // 16], U16, name="offs_sb")
         pos1_sb = keep.tile([P, T // 16], U16, name="pos1_sb")
         pos2_sb = keep.tile([P, T // 16], U16, name="pos2_sb")
-        gate_first = keep.tile([P, C], F32, name="gate_first")
-        gate_rest = keep.tile([P, S - C], F32, name="gate_rest")
-        tokens = [[keep.tile([P, T], F32, name=f"tokens{a}{j}") for j in range(PACK)] for a in range(PASSES)]
+        gate_first = keep.tile([P, GS], F32, name="gate_first")
+        gate_rest = keep.tile([P, S - GS], F32, name="gate_rest")
+        tokens = [[keep.tile([P, TW], F32, name=f"tokens{a}{j}") for j in range(PACK)] for a in range(PASSES)]
         y_sb = keep.tile([P, N // P, S], F32, name="y_sb")
         x_rows = xT.rearrange("(a p j) t -> a j p t", p=P, j=PACK)
+        x_bf = keep.tile([P, PASSES, PACK * S], BF16, name="x_bf", align_bytes=64)
+        x_codes = keep.tile([P, PASSES, S], U32, name="x_codes", align_bytes=64)
+        x_scales = keep.tile([P, PASSES, S], U8, name="x_scales", align_bytes=64)
         t = {}
 
         def gate_cols(lo, hi):
-            return gate_first[:, lo:hi] if lo < C else gate_rest[:, lo - C : hi - C]
+            return gate_first[:, lo:hi] if lo < GS else gate_rest[:, lo - GS : hi - GS]
 
         def quantize2(key, tag, width, values, a):
             if key not in t:
@@ -98,56 +103,59 @@ def tile_moe_pre_glu_silu_kernel(tc, xT, w1, w3, w2, gate, offs, pos1, pos2, out
                 nc.sync.dma_start(out=pos2_sb[:], in_=pos2)
             elif k == "lg":
                 if r[0] == 0:
-                    nc.sync.dma_start(out=gate_first[:], in_=gate[0:P, 0:C])
+                    nc.sync.dma_start(out=gate_first[:], in_=gate[0:P, 0:GS])
                 else:
-                    nc.sync.dma_start(out=gate_rest[:], in_=gate[0:P, C:S])
+                    nc.sync.dma_start(out=gate_rest[:], in_=gate[0:P, GS:S])
             elif k == "lx":
-                nc.sync.dma_start(out=tokens[r[0]][r[1]][:], in_=x_rows[r[0], r[1]])
+                nc.sync.dma_start(out=tokens[r[0]][r[1]][:, 0:T], in_=x_rows[r[0], r[1]])
             elif k == "lw":
                 e, m, a = r
                 t[("raw", e, m, a)] = ring.tile([P, PACK, H], F32, name="w_raw", bufs=B["wraw"])
                 src = (w1, w3)[m][e, a * K_PASS : (a + 1) * K_PASS, :]
                 nc.sync.dma_start(out=t[("raw", e, m, a)][:], in_=src.rearrange("(p j) c -> p j c", j=PACK))
             elif k == "lw2":
-                e = r[0]
-                t[("raw2", e)] = ring.tile([P, PACK, N], F32, name="w2_raw", tag="w_raw", bufs=B["wraw"])
-                nc.sync.dma_start(out=t[("raw2", e)][:], in_=w2[e].rearrange("(p j) c -> p j c", j=PACK))
+                e, e1 = r
+                t[("raw2", e)] = ring.tile([P, e1 - e, PACK, N], F32, name="w2_raw", tag="w_raw", bufs=B["wraw"])
+                nc.sync.dma_start(out=t[("raw2", e)][:], in_=w2[e:e1].rearrange("e (p j) c -> p e j c", j=PACK))
             elif k == "G":
-                e0, e1, a, j, md = r
+                lo, hi, a, j, md = r
                 if j == 0:
-                    picked = ring.tile([P, PACK, (e1 - e0) * C], F32, name=f"x_picked{e1 - e0}", bufs=B[f"xp{e1 - e0}"])
-                    t[("xg", e0, a)] = picked
-                    for e in range(e0, e1):
-                        t[("xp", e, a)] = picked[:, :, (e - e0) * C : (e - e0 + 1) * C]
-                window = tokens[a][j][:].indirect(offs_sb[:, e0 * C // 16 : e1 * C // 16])
+                    picked = ring.tile([P, PACK, (hi - lo) * HALF], F32, name=f"x_picked{hi - lo}", bufs=B[f"xp{hi - lo}"])
+                    for u in range(lo, hi):
+                        t[("xp", u, a)] = (picked, lo)
+                picked = t[("xp", lo, a)][0]
+                window = tokens[a][j][:].indirect(offs_sb[:, lo * HALF // 16 : hi * HALF // 16])
                 if md == "c":
-                    nc.vector.tensor_tensor(t[("xg", e0, a)][:, j, :], window, gate_cols(e0 * C, e1 * C), MULT)
+                    nc.vector.tensor_tensor(picked[:, j, :], window, gate_cols(lo * HALF, hi * HALF), MULT)
                 else:
-                    nc.vector.tensor_copy(t[("xg", e0, a)][:, j, :], window)
+                    nc.vector.tensor_copy(picked[:, j, :], window)
             elif k == "cx":
-                e, a, en = r
-                if ("xbf", e) not in t:
-                    t[("xbf", e)] = ring.tile([P, PASSES, PACK * C], BF16, name="x_bf", bufs=B["xbf"], align_bytes=64)
+                lo, hi, a, en = r
+                picked, base = t[("xp", lo, a)]
+                src = picked[:, :, (lo - base) * HALF : (hi - base) * HALF]
+                dst = x_bf[:, a, PACK * HALF * lo : PACK * HALF * hi]
                 if en == "G":
-                    for half in range(2):
-                        lo, hi = half * HALF, (half + 1) * HALF
-                        nc.gpsimd.tensor_tensor(
-                            t[("xbf", e)][:, a, PACK * lo : PACK * hi].rearrange("p (s j) -> p s j", j=PACK),
-                            t[("xp", e, a)][:, :, lo:hi].rearrange("p j s -> p s j"),
-                            gate_cols(e * C + lo, e * C + hi).unsqueeze(2).to_broadcast([P, HALF, PACK]),
-                            MULT,
-                        )
+                    nc.gpsimd.tensor_tensor(
+                        dst.rearrange("p (s j) -> p s j", j=PACK),
+                        src.rearrange("p j s -> p s j"),
+                        gate_cols(lo * HALF, hi * HALF).unsqueeze(2).to_broadcast([P, (hi - lo) * HALF, PACK]),
+                        MULT,
+                    )
                 else:
-                    interleave(en, t[("xbf", e)][:, a, :], t[("xp", e, a)])
+                    interleave(en, dst, src)
             elif k == "qx":
-                e, a = r
-                quantize2(("xq", e), "xq", C, t[("xbf", e)], a)
+                lo, hi, a = r
+                nc.vector.quantize_mx(
+                    out=x_codes[:, a, lo * HALF : hi * HALF].bitcast(FP8X4),
+                    scales=x_scales[:, a, lo * HALF : hi * HALF],
+                    in_=x_bf[:, a, PACK * HALF * lo : PACK * HALF * hi],
+                )
             elif k == "cw":
                 e, m, a, tp, en = r
                 if ("wbf", e, m) not in t:
                     t[("wbf", e, m)] = ring.tile([P, PASSES, PACK * H], BF16, name="w_bf", bufs=B["wbf"], align_bytes=64)
-                dst = t[("wbf", e, m)][:, a, :].rearrange("p (tp t2 q j) -> p tp q j t2", tp=2, t2=2, j=PACK)
-                src = t[("raw", e, m, a)][:].rearrange("p j (q tp t2) -> p tp q j t2", tp=2, t2=2)
+                dst = t[("wbf", e, m)][:, a, :].rearrange("p (t h q j) -> p h q j t", t=PACK, h=2, j=PACK)
+                src = t[("raw", e, m, a)][:].rearrange("p j (h q t) -> p h q j t", t=PACK, h=2)
                 if tp is None:
                     cast(en, dst, src)
                 else:
@@ -156,21 +164,28 @@ def tile_moe_pre_glu_silu_kernel(tc, xT, w1, w3, w2, gate, offs, pos1, pos2, out
                 e, m, a = r
                 quantize2(("wq", e, m), "wq", H, t[("wbf", e, m)], a)
             elif k == "cw2":
-                e, en = r
-                t[("w2bf", e)] = ring.tile([P, PACK * N], BF16, name="w2_bf", bufs=B["w2bf"], align_bytes=64)
-                interleave(en, t[("w2bf", e)][:], t[("raw2", e)][:])
+                e, e1, en = r
+                t[("w2bf", e)] = ring.tile([P, (e1 - e) * PACK * N], BF16, name="w2_bf", bufs=B["w2bf"], align_bytes=64)
+                cast(
+                    en,
+                    t[("w2bf", e)][:].rearrange("p (e c i j) -> p e c j i", e=e1 - e, i=4, j=PACK),
+                    t[("raw2", e)][:].rearrange("p e j (c i) -> p e c j i", i=4),
+                )
             elif k == "qw2":
-                t[("w2q",) + r] = quantize("w2q", N, t[("w2bf",) + r][:])
+                e, e1 = r
+                codes, scales = quantize("w2q", (e1 - e) * N, t[("w2bf", e)][:])
+                for x in range(e, e1):
+                    t[("w2q", x)] = (codes[:, (x - e) * N : (x - e + 1) * N], scales[:, (x - e) * N : (x - e + 1) * N])
             elif k == "mm":
                 e, m, half = r
                 bank = psum.tile([P, PACK, HALF], F32, name=f"bank{m}", bufs=3)
                 t[("b",) + r] = bank
-                slots = slice(half * HALF, (half + 1) * HALF)
+                slots = slice(e * C + half * HALF, e * C + (half + 1) * HALF)
                 for u in range(PACK):
                     cols = slice(u * P, (u + 1) * P)
                     for a in range(PASSES):
                         wq = t[("wq", e, m)]
-                        xq = t[("xq", e)]
+                        xq = (x_codes, x_scales)
                         nc.tensor.matmul_mx(
                             out=bank[:, u, :],
                             lhsT=wq[0][:, a, cols].bitcast(FP8X4),

@@ -8,10 +8,38 @@ P = 128
 PACK = 4
 K_PASS = P * PACK
 PASSES = K // K_PASS
-HALF = 128
+MATRICES = 2 * E
+BANK_SLOTS = 128
+LIST_ROWS = 16
 
 FLOPS = 2 * S * (2 * K * H + H * N)
-BYTES = 4 * (K * T + E * (2 * K * H + H * N) + S + N * T) + 2 * P * (S + 2 * T) // 16
+BYTES = 4 * (K * T + E * (2 * K * H + H * N) + S + N * T) + 2 * P * (S + 2 * T) // LIST_ROWS
+
+WINDOW = T + 32
+SLOT_HALVES = ((0, S // 2), (S // 2, S))
+TAIL_SLOT = S - BANK_SLOTS
+X_ROUND = ((0, TAIL_SLOT, S, True), (1, 0, S // 2, True), (1, S // 2, S, True), (0, S // 2, TAIL_SLOT, False))
+X_QUANTISE = (((0, 4 * C), (4 * C, S)), ((0, C), (C, S)))
+CHUNKS_BEFORE_TOKENS = (0, 0, 0, 3, 4, 4, 4, 11)
+VECTOR_HALVES = {(1, 1): 1, (5, 1): 1, (6, 0): 2, (7, 1): 2, (8, 0): 2, (9, 1): 2}
+SPLIT_MATRIX = 1
+CHUNKS_BEFORE_POS = 13
+SILU_LAG = 4
+HIDDEN_LAG = 6
+EARLY, MIDDLE, LAST = (0, 2), (2, 4), (4, 5)
+COMBINE_PLAN = (
+    (((0, T), True),),
+    (((0, T // 2), True), ((T // 2, T), False)),
+)
+
+RAW_BUFS = 7
+PICKED_BUFS = 2
+ROUNDED_BUFS = 3
+CODE_BUFS = 4
+SILU_BUFS = 6
+H_BUFS = 2
+FIRST_BANKS = 3
+Y_BANKS = 2
 
 F32 = mybir.dt.float32
 BF16 = mybir.dt.bfloat16
@@ -23,223 +51,272 @@ MULT = mybir.AluOpType.mult
 ADD = mybir.AluOpType.add
 SILU = mybir.ActivationFunctionType.Silu
 
-ORDER = [('lx', 0, 0), ('lo',), ('lg', 0), ('lx', 0, 1), ('lg', 1), ('lx', 0, 2), ('lw', 0, 0, 0), ('lw', 0, 0, 1), ('lw', 0, 1, 0), ('lx', 0, 3), ('lx', 1, 0), ('lx', 1, 1), ('lw', 0, 1, 1), ('lw', 1, 0, 0), ('lx', 1, 2), ('lw', 1, 0, 1), ('lw', 1, 1, 0), ('lw', 1, 1, 1), ('lw', 2, 0, 0), ('lw', 2, 0, 1), ('lw', 2, 1, 0), ('lx', 1, 3), ('lw', 2, 1, 1), ('lw', 3, 0, 0), ('lw', 3, 0, 1), ('lw', 3, 1, 0), ('lp',), ('lw', 3, 1, 1), ('lw', 4, 0, 0), ('lw', 4, 0, 1), ('lw', 4, 1, 0), ('lw2', 0, 2), ('lw', 4, 1, 1), ('lw2', 2, 4), ('lw2', 4, 5), ('G', 0, 2, 0, 0, 'c'), ('G', 0, 2, 0, 1, 'c'), ('G', 0, 2, 0, 2, 'c'), ('G', 0, 2, 0, 3, 'c'), ('G', 2, 6, 0, 0, 'c'), ('G', 2, 6, 0, 1, 'c'), ('G', 2, 6, 0, 2, 'c'), ('G', 2, 6, 0, 3, 'c'), ('cx', 0, 2, 0, 'S'), ('cx', 2, 6, 0, 'S'), ('G', 0, 2, 1, 0, 'c'), ('G', 0, 2, 1, 1, 'c'), ('G', 0, 2, 1, 2, 'c'), ('G', 0, 2, 1, 3, 'c'), ('G', 6, 10, 0, 0, 'c'), ('G', 6, 10, 0, 1, 'c'), ('G', 6, 10, 0, 2, 'c'), ('G', 6, 10, 0, 3, 'c'), ('cx', 0, 2, 1, 'V'), ('cx', 6, 10, 0, 'S'), ('G', 2, 6, 1, 0, 'c'), ('G', 2, 6, 1, 1, 'c'), ('G', 2, 6, 1, 2, 'c'), ('G', 2, 6, 1, 3, 'c'), ('cx', 2, 6, 1, 'V'), ('G', 6, 10, 1, 0, 'c'), ('G', 6, 10, 1, 1, 'c'), ('G', 6, 10, 1, 2, 'c'), ('G', 6, 10, 1, 3, 'c'), ('cx', 6, 10, 1, 'S'), ('qx', 0, 2, 0), ('cw2', 0, 2, 'V'), ('qw2', 0, 2), ('qx', 0, 2, 1), ('cw', 0, 0, 0, None, 'S'), ('cw', 0, 0, 1, None, 'S'), ('qx', 2, 10, 0), ('cw', 0, 1, 0, None, 'S'), ('cw', 0, 1, 1, None, 'S'), ('cw', 1, 0, 0, None, 'S'), ('qw', 0, 0, None), ('mm', 0, 0, 0), ('mm', 0, 0, 1), ('cw', 1, 0, 1, None, 'S'), ('qx', 2, 6, 1), ('cw', 1, 1, 0, None, 'S'), ('qw', 0, 1, None), ('mm', 0, 1, 0), ('mm', 0, 1, 1), ('cw', 1, 1, 1, None, 'V'), ('cw', 2, 0, 0, None, 'S'), ('qw', 1, 0, None), ('mm', 1, 0, 0), ('mm', 1, 0, 1), ('cw', 2, 0, 1, None, 'S'), ('qx', 6, 10, 1), ('cw', 2, 1, 0, None, 'S'), ('qw', 1, 1, None), ('mm', 1, 1, 0), ('mm', 1, 1, 1), ('cw', 2, 1, 1, 0, 'S'), ('cw', 2, 1, 1, 1, 'V'), ('cw', 3, 0, 0, None, 'V'), ('silu', 0, 0), ('silu', 0, 1), ('h', 0, 0), ('h', 0, 1), ('qw', 2, 0, None), ('mm', 2, 0, 0), ('mm', 2, 0, 1), ('qh', 0), ('mmy', 0), ('cw', 3, 0, 1, None, 'S'), ('cy', 0), ('cw', 3, 1, 0, None, 'S'), ('qw', 2, 1, None), ('mm', 2, 1, 0), ('mm', 2, 1, 1), ('cw', 3, 1, 1, None, 'V'), ('cw', 4, 0, 0, 0, 'S'), ('cw', 4, 0, 0, 1, 'V'), ('silu', 1, 0), ('silu', 1, 1), ('h', 1, 0), ('h', 1, 1), ('qw', 3, 0, None), ('mm', 3, 0, 0), ('mm', 3, 0, 1), ('qh', 1), ('mmy', 1), ('cw', 4, 0, 1, None, 'S'), ('cy', 1), ('cw', 4, 1, 0, None, 'S'), ('qw', 3, 1, None), ('mm', 3, 1, 0), ('mm', 3, 1, 1), ('cw', 4, 1, 1, None, 'V'), ('silu', 2, 0), ('silu', 2, 1), ('h', 2, 0), ('h', 2, 1), ('qw', 4, 0, None), ('mm', 4, 0, 0), ('mm', 4, 0, 1), ('qh', 2), ('qw', 4, 1, None), ('mm', 4, 1, 0), ('mm', 4, 1, 1), ('silu', 3, 0), ('silu', 3, 1), ('h', 3, 0), ('h', 3, 1), ('qh', 3), ('cw2', 2, 4, 'S'), ('qw2', 2, 4), ('mmy', 2), ('mmy', 3), ('cy', 2), ('cy', 3), ('silu', 4, 0), ('silu', 4, 1), ('h', 4, 0), ('h', 4, 1), ('qh', 4), ('cw2', 4, 5, 'V'), ('qw2', 4, 5), ('mmy', 4), ('cy', 4), ('tail', 0, 0, 640, 'G'), ('tail', 1, 0, 320, 'G'), ('tail', 1, 320, 640, 'V')]
-B = {"wraw":7,"wbf":4,"wq":4,"w2q":3,"w2bf":2,"xp2":1,"xp4":2,"silu":5,"hq":2,"gs":2}
-GS = B["gs"] * HALF
-TW = T + 0
-
 
 def tile_moe_pre_glu_silu_kernel(tc, xT, w1, w3, w2, gate, offs, pos1, pos2, out):
     nc = tc.nc
 
-    def cast(engine, dst, src):
-        if engine == "S":
-            nc.scalar.copy(out=dst, in_=src)
-        elif engine == "G":
-            nc.gpsimd.tensor_scalar(dst, src, 1.0, 0.0, MULT, ADD)
-        else:
+    def round_copy(on_vector, dst, src):
+        if on_vector:
             nc.vector.tensor_copy(out=dst, in_=src)
+        else:
+            nc.scalar.copy(out=dst, in_=src)
 
-    def interleave(engine, rounded, src):
-        cast(
-            engine,
-            rounded.rearrange("p (c i j) -> p c j i", i=4, j=PACK),
-            src.rearrange("p j (c i) -> p c j i", i=4),
+    def quantize(codes, scales, values):
+        nc.vector.quantize_mx(out=codes.bitcast(FP8X4), scales=scales, in_=values)
+
+    def multiply(bank, stationary, stationary_scales, moving, moving_scales, start, stop):
+        nc.tensor.matmul_mx(
+            out=bank,
+            lhsT=stationary.bitcast(FP8X4),
+            lhsT_scale=stationary_scales,
+            rhs=moving.bitcast(FP8X4),
+            rhs_scale=moving_scales,
+            start=start,
+            stop=stop,
         )
+
+    def list_columns(lo, hi):
+        return slice(lo // LIST_ROWS, hi // LIST_ROWS)
 
     with ExitStack() as ctx:
         keep = ctx.enter_context(tc.tile_pool(name="keep", bufs=1))
-        ring = ctx.enter_context(tc.tile_pool(name="ring", bufs=2))
+        ring = ctx.enter_context(tc.tile_pool(name="ring", bufs=1))
         psum = ctx.enter_context(tc.psum_pool(name="psum", bufs=1))
 
-        offs_sb = keep.tile([P, S // 16], U16, name="offs_sb")
-        pos1_sb = keep.tile([P, T // 16], U16, name="pos1_sb")
-        pos2_sb = keep.tile([P, T // 16], U16, name="pos2_sb")
-        gate_first = keep.tile([P, GS], F32, name="gate_first")
-        gate_rest = keep.tile([P, S - GS], F32, name="gate_rest")
-        tokens = [[keep.tile([P, TW], F32, name=f"tokens{a}{j}") for j in range(PACK)] for a in range(PASSES)]
-        y_sb = keep.tile([P, N // P, S], F32, name="y_sb")
-        x_rows = xT.rearrange("(a p j) t -> a j p t", p=P, j=PACK)
-        x_bf = keep.tile([P, PASSES, PACK * S], BF16, name="x_bf", align_bytes=64)
+        offs_sb = keep.tile([P, S // LIST_ROWS], U16, name="offs_sb")
+        pos1_sb = keep.tile([P, T // LIST_ROWS], U16, name="pos1_sb")
+        pos2_sb = keep.tile([P, T // LIST_ROWS], U16, name="pos2_sb")
+        gate_sb = [keep.tile([P, hi - lo], F32, name=f"gate{lo}") for lo, hi in SLOT_HALVES]
+        tokens = [keep.tile([P, WINDOW], F32, name=f"tokens{tile}") for tile in range(PASSES * PACK)]
+        x_rounded = keep.tile([P, PASSES, PACK * S], BF16, name="x_rounded", align_bytes=64)
         x_codes = keep.tile([P, PASSES, S], U32, name="x_codes", align_bytes=64)
         x_scales = keep.tile([P, PASSES, S], U8, name="x_scales", align_bytes=64)
-        t = {}
+        w2_rounded = keep.tile([P, N // P, E, PACK * P], BF16, name="w2_rounded", align_bytes=64)
+        w2_codes = keep.tile([P, N // P, E, P], U32, name="w2_codes", align_bytes=64)
+        w2_scales = keep.tile([P, N // P, E, P], U8, name="w2_scales", align_bytes=64)
+        y_sb = [keep.tile([P, S], F32, name=f"y_sb{g}") for g in range(N // P)]
 
-        def gate_cols(lo, hi):
-            return gate_first[:, lo:hi] if lo < GS else gate_rest[:, lo - GS : hi - GS]
+        def raw_tile(shape, name):
+            return ring.tile(shape, F32, name=name, tag="raw", bufs=RAW_BUFS)
 
-        def quantize2(key, tag, width, values, a):
-            if key not in t:
-                codes = ring.tile([P, PASSES, width], U32, name=tag + "_codes", bufs=B[tag], align_bytes=64)
-                scales = ring.tile([P, PASSES, width], U8, name=tag + "_scales", bufs=B[tag], align_bytes=64)
-                t[key] = (codes, scales)
-            codes, scales = t[key]
-            if a is None:
-                flat = "p a c -> p (a c)"
-                nc.vector.quantize_mx(
-                    out=codes[:].rearrange(flat).bitcast(FP8X4), scales=scales[:].rearrange(flat), in_=values[:].rearrange(flat)
-                )
-            else:
-                nc.vector.quantize_mx(out=codes[:, a, :].bitcast(FP8X4), scales=scales[:, a, :], in_=values[:, a, :])
+        for tile in tokens:
+            nc.gpsimd.memset(tile[:, T:WINDOW], 0.0)
+        token_rows = xT.rearrange("(a p j) t -> a j p t", p=P, j=PACK)
+        chunks = [(matrix, a) for matrix in range(MATRICES) for a in range(PASSES)]
+        w_raw = {}
 
-        def quantize(tag, width, values):
-            codes = ring.tile([P, width], U32, name=tag + "_codes", bufs=B[tag], align_bytes=64)
-            scales = ring.tile([P, width], U8, name=tag + "_scales", bufs=B[tag], align_bytes=64)
-            nc.vector.quantize_mx(out=codes[:].bitcast(FP8X4), scales=scales[:], in_=values)
-            return codes, scales
+        def load_tokens(tile):
+            nc.sync.dma_start(out=tokens[tile][:, 0:T], in_=token_rows[tile // PACK, tile % PACK])
 
-        warm_in = keep.tile([P, 1], F32, name="warm_in")
-        warm_out = keep.tile([P, 1], F32, name="warm_out")
-        nc.vector.memset(warm_in[:], 0.0)
-        nc.scalar.activation(out=warm_out[:], in_=warm_in[:], func=SILU)
-
-        for step in ORDER:
-            k = step[0]
-            r = tuple(step[1:])
-            if k == "lo":
-                nc.sync.dma_start(out=offs_sb[:], in_=offs)
-            elif k == "lp":
+        load_tokens(0)
+        nc.sync.dma_start(out=offs_sb[:], in_=offs)
+        for half, (lo, hi) in reversed(list(enumerate(SLOT_HALVES))):
+            nc.sync.dma_start(out=gate_sb[half][:], in_=gate[0:P, lo:hi])
+        for loaded, (matrix, a) in enumerate(chunks):
+            for tile in range(1, PASSES * PACK):
+                if CHUNKS_BEFORE_TOKENS[tile] == loaded:
+                    load_tokens(tile)
+            if loaded == CHUNKS_BEFORE_POS:
                 nc.sync.dma_start(out=pos1_sb[:], in_=pos1)
                 nc.sync.dma_start(out=pos2_sb[:], in_=pos2)
-            elif k == "lg":
-                if r[0] == 0:
-                    nc.sync.dma_start(out=gate_first[:], in_=gate[0:P, 0:GS])
-                else:
-                    nc.sync.dma_start(out=gate_rest[:], in_=gate[0:P, GS:S])
-            elif k == "lx":
-                nc.sync.dma_start(out=tokens[r[0]][r[1]][:, 0:T], in_=x_rows[r[0], r[1]])
-            elif k == "lw":
-                e, m, a = r
-                t[("raw", e, m, a)] = ring.tile([P, PACK, H], F32, name="w_raw", bufs=B["wraw"])
-                src = (w1, w3)[m][e, a * K_PASS : (a + 1) * K_PASS, :]
-                nc.sync.dma_start(out=t[("raw", e, m, a)][:], in_=src.rearrange("(p j) c -> p j c", j=PACK))
-            elif k == "lw2":
-                e, e1 = r
-                t[("raw2", e)] = ring.tile([P, e1 - e, PACK, N], F32, name="w2_raw", tag="w_raw", bufs=B["wraw"])
-                nc.sync.dma_start(out=t[("raw2", e)][:], in_=w2[e:e1].rearrange("e (p j) c -> p e j c", j=PACK))
-            elif k == "G":
-                lo, hi, a, j, md = r
-                if j == 0:
-                    picked = ring.tile([P, PACK, (hi - lo) * HALF], F32, name=f"x_picked{hi - lo}", bufs=B[f"xp{hi - lo}"])
-                    for u in range(lo, hi):
-                        t[("xp", u, a)] = (picked, lo)
-                picked = t[("xp", lo, a)][0]
-                window = tokens[a][j][:].indirect(offs_sb[:, lo * HALF // 16 : hi * HALF // 16])
-                if md == "c":
-                    nc.vector.tensor_tensor(picked[:, j, :], window, gate_cols(lo * HALF, hi * HALF), MULT)
-                else:
-                    nc.vector.tensor_copy(picked[:, j, :], window)
-            elif k == "cx":
-                lo, hi, a, en = r
-                picked, base = t[("xp", lo, a)]
-                src = picked[:, :, (lo - base) * HALF : (hi - base) * HALF]
-                dst = x_bf[:, a, PACK * HALF * lo : PACK * HALF * hi]
-                if en == "G":
-                    nc.gpsimd.tensor_tensor(
-                        dst.rearrange("p (s j) -> p s j", j=PACK),
-                        src.rearrange("p j s -> p s j"),
-                        gate_cols(lo * HALF, hi * HALF).unsqueeze(2).to_broadcast([P, (hi - lo) * HALF, PACK]),
-                        MULT,
-                    )
-                else:
-                    interleave(en, dst, src)
-            elif k == "qx":
-                lo, hi, a = r
-                nc.vector.quantize_mx(
-                    out=x_codes[:, a, lo * HALF : hi * HALF].bitcast(FP8X4),
-                    scales=x_scales[:, a, lo * HALF : hi * HALF],
-                    in_=x_bf[:, a, PACK * HALF * lo : PACK * HALF * hi],
+            rows = (w1, w3)[matrix % 2][matrix // 2, a * K_PASS : (a + 1) * K_PASS, :]
+            w_raw[(matrix, a)] = raw_tile([P, PACK, H], "w_raw")
+            nc.sync.dma_start(out=w_raw[(matrix, a)][:], in_=rows.rearrange("(p j) c -> p j c", j=PACK))
+        w2_raw = {}
+        for e0, e1 in (EARLY, MIDDLE, LAST):
+            w2_raw[e0] = raw_tile([P, e1 - e0, PACK, N], "w2_raw")
+            nc.sync.dma_start(out=w2_raw[e0][:], in_=w2[e0:e1].rearrange("e (p j) c -> p e j c", j=PACK))
+
+        picked = {}
+
+        def gather_x(a, half):
+            lo, hi = SLOT_HALVES[half]
+            picked[(a, half)] = ring.tile([P, PACK, hi - lo], F32, name="picked", bufs=PICKED_BUFS)
+            for j in range(PACK):
+                window = tokens[a * PACK + j][:].indirect(offs_sb[:, list_columns(lo, hi)])
+                nc.vector.tensor_tensor(picked[(a, half)][:, j, :], window, gate_sb[half][:], MULT)
+
+        def round_x(a, lo, hi, on_vector):
+            half = lo // (S // 2)
+            base = SLOT_HALVES[half][0]
+            round_copy(
+                on_vector,
+                x_rounded[:, a, PACK * lo : PACK * hi].rearrange("p (c i j) -> p c j i", i=4, j=PACK),
+                picked[(a, half)][:, :, lo - base : hi - base].rearrange("p j (c i) -> p c j i", i=4),
+            )
+
+        def quantize_x(a, lo, hi):
+            quantize(x_codes[:, a, lo:hi], x_scales[:, a, lo:hi], x_rounded[:, a, PACK * lo : PACK * hi])
+
+        w_rounded = {}
+        w_quantized = {}
+        banks = {}
+        activated = {}
+        h_quantized = {}
+
+        def round_chunk(matrix, a):
+            if a == 0:
+                w_rounded[matrix] = ring.tile(
+                    [P, PASSES, PACK * H], BF16, name="w_rounded", bufs=ROUNDED_BUFS, align_bytes=64
                 )
-            elif k == "cw":
-                e, m, a, tp, en = r
-                if ("wbf", e, m) not in t:
-                    t[("wbf", e, m)] = ring.tile([P, PASSES, PACK * H], BF16, name="w_bf", bufs=B["wbf"], align_bytes=64)
-                dst = t[("wbf", e, m)][:, a, :].rearrange("p (t h q j) -> p h q j t", t=PACK, h=2, j=PACK)
-                src = t[("raw", e, m, a)][:].rearrange("p j (h q t) -> p h q j t", t=PACK, h=2)
-                if tp is None:
-                    cast(en, dst, src)
-                else:
-                    cast(en, dst[:, tp], src[:, tp])
-            elif k == "qw":
-                e, m, a = r
-                quantize2(("wq", e, m), "wq", H, t[("wbf", e, m)], a)
-            elif k == "cw2":
-                e, e1, en = r
-                t[("w2bf", e)] = ring.tile([P, (e1 - e) * PACK * N], BF16, name="w2_bf", bufs=B["w2bf"], align_bytes=64)
-                cast(
-                    en,
-                    t[("w2bf", e)][:].rearrange("p (e c i j) -> p e c j i", e=e1 - e, i=4, j=PACK),
-                    t[("raw2", e)][:].rearrange("p e j (c i) -> p e c j i", i=4),
-                )
-            elif k == "qw2":
-                e, e1 = r
-                codes, scales = quantize("w2q", (e1 - e) * N, t[("w2bf", e)][:])
-                for x in range(e, e1):
-                    t[("w2q", x)] = (codes[:, (x - e) * N : (x - e + 1) * N], scales[:, (x - e) * N : (x - e + 1) * N])
-            elif k == "mm":
-                e, m, half = r
-                bank = psum.tile([P, PACK, HALF], F32, name=f"bank{m}", bufs=3)
-                t[("b",) + r] = bank
-                slots = slice(e * C + half * HALF, e * C + (half + 1) * HALF)
+            dst = w_rounded[matrix][:, a, :].rearrange("p (u q j) -> p q j u", u=PACK, j=PACK)
+            src = w_raw[(matrix, a)][:].rearrange("p j (q u) -> p q j u", u=PACK)
+            split = P - VECTOR_HALVES.get((matrix, a), 0) * P // 2
+            if split > 0:
+                round_copy(False, dst[:, 0:split], src[:, 0:split])
+            if split < P:
+                round_copy(True, dst[:, split:P], src[:, split:P])
+
+        def quantize_matrix(matrix, a0, a1):
+            if a0 == 0:
+                codes = ring.tile([P, PASSES, H], U32, name="w_codes", bufs=CODE_BUFS, align_bytes=64)
+                scales = ring.tile([P, PASSES, H], U8, name="w_scales", bufs=CODE_BUFS, align_bytes=64)
+                w_quantized[matrix] = (codes, scales)
+            codes, scales = w_quantized[matrix]
+            flat = "p a c -> p (a c)"
+            quantize(
+                codes[:, a0:a1, :].rearrange(flat),
+                scales[:, a0:a1, :].rearrange(flat),
+                w_rounded[matrix][:, a0:a1, :].rearrange(flat),
+            )
+
+        def multiply_matrix(matrix):
+            codes, scales = w_quantized[matrix]
+            for part in range(C // BANK_SLOTS):
+                bank = psum.tile([P, PACK, BANK_SLOTS], F32, name=f"first_bank{matrix % 2}", bufs=FIRST_BANKS)
+                banks[(matrix, part)] = bank
+                first_slot = (matrix // 2) * C + part * BANK_SLOTS
+                slots = slice(first_slot, first_slot + BANK_SLOTS)
                 for u in range(PACK):
                     cols = slice(u * P, (u + 1) * P)
                     for a in range(PASSES):
-                        wq = t[("wq", e, m)]
-                        xq = (x_codes, x_scales)
-                        nc.tensor.matmul_mx(
-                            out=bank[:, u, :],
-                            lhsT=wq[0][:, a, cols].bitcast(FP8X4),
-                            lhsT_scale=wq[1][:, a, cols],
-                            rhs=xq[0][:, a, slots].bitcast(FP8X4),
-                            rhs_scale=xq[1][:, a, slots],
-                            start=(a == 0),
-                            stop=(a == PASSES - 1),
+                        multiply(
+                            bank[:, u, :],
+                            codes[:, a, cols],
+                            scales[:, a, cols],
+                            x_codes[:, a, slots],
+                            x_scales[:, a, slots],
+                            a == 0,
+                            a == PASSES - 1,
                         )
-            elif k == "silu":
-                e, half = r
-                t[("s",) + r] = ring.tile([P, HALF, PACK], F32, name="silu", bufs=B["silu"])
-                nc.scalar.activation(out=t[("s",) + r][:], in_=t[("b", e, 0, half)][:].rearrange("p u s -> p s u"), func=SILU)
-            elif k == "h":
-                e, half = r
-                if ("h", e) not in t:
-                    t[("h", e)] = ring.tile([P, C, PACK], BF16, name="h", bufs=2, align_bytes=64)
+
+        def activate(e):
+            for part in range(C // BANK_SLOTS):
+                silu = ring.tile([P, BANK_SLOTS, PACK], F32, name="silu", bufs=SILU_BUFS)
+                nc.scalar.activation(out=silu[:], in_=banks[(2 * e, part)][:].rearrange("p u s -> p s u"), func=SILU)
+                activated[(e, part)] = silu
+
+        def make_hidden(e):
+            h = ring.tile([P, C, PACK], BF16, name="h", bufs=H_BUFS, align_bytes=64)
+            for part in range(C // BANK_SLOTS):
                 nc.vector.tensor_tensor(
-                    t[("h", e)][:, half * HALF : (half + 1) * HALF, :],
-                    t[("b", e, 1, half)][:].rearrange("p u s -> p s u"),
-                    t[("s", e, half)][:],
+                    h[:, part * BANK_SLOTS : (part + 1) * BANK_SLOTS, :],
+                    banks[(2 * e + 1, part)][:].rearrange("p u s -> p s u"),
+                    activated[(e, part)][:],
                     MULT,
                 )
-            elif k == "qh":
-                t[("hq",) + r] = quantize("hq", C, t[("h",) + r][:].rearrange("p s u -> p (s u)"))
-            elif k == "mmy":
-                e = r[0]
-                bank = psum.tile([P, N // P, C], F32, name="bank_y", bufs=2)
-                t[("by", e)] = bank
-                for g in range(N // P):
-                    cols = slice(g * P, (g + 1) * P)
-                    nc.tensor.matmul_mx(
-                        out=bank[:, g, :],
-                        lhsT=t[("w2q", e)][0][:, cols].bitcast(FP8X4),
-                        lhsT_scale=t[("w2q", e)][1][:, cols],
-                        rhs=t[("hq", e)][0][:].bitcast(FP8X4),
-                        rhs_scale=t[("hq", e)][1][:],
-                        start=True,
-                        stop=True,
-                    )
-            elif k == "cy":
-                e = r[0]
-                if e + 1 < E:
-                    nc.scalar.copy(out=y_sb[:, :, e * C : (e + 1) * C], in_=t[("by", e)][:])
-                else:
-                    for g in range(N // P):
-                        nc.scalar.copy(out=y_sb[:, g, e * C : (e + 1) * C], in_=t[("by", e)][:, g, :])
-            elif k == "tail":
-                g, lo, hi, en = r
-                first = ring.tile([P, hi - lo], F32, name="first", tag="w_raw", bufs=B["wraw"])
-                second = ring.tile([P, hi - lo], F32, name="second", tag="w_raw", bufs=B["wraw"])
-                total = ring.tile([P, hi - lo], F32, name="total", tag="w_raw", bufs=B["wraw"])
-                cols = slice(lo // 16, hi // 16)
-                nc.vector.tensor_copy(first[:], y_sb[:, g, :].indirect(pos1_sb[:, cols]))
-                nc.vector.tensor_copy(second[:], y_sb[:, g, :].indirect(pos2_sb[:, cols]))
-                (nc.vector if en == "V" else nc.gpsimd).tensor_tensor(total[:], first[:], second[:], ADD)
+            codes = ring.tile([P, C], U32, name="h_codes", bufs=E, align_bytes=64)
+            scales = ring.tile([P, C], U8, name="h_scales", bufs=E, align_bytes=64)
+            quantize(codes[:], scales[:], h[:].rearrange("p s u -> p (s u)"))
+            h_quantized[e] = (codes, scales)
+
+        y_banks = {}
+
+        def round_w2(g, experts, on_vector):
+            e0, e1 = experts
+            round_copy(
+                on_vector,
+                w2_rounded[:, g, e0:e1, :].rearrange("p e (c i j) -> p e c j i", i=4, j=PACK),
+                w2_raw[e0][:, :, :, g * P : (g + 1) * P].rearrange("p e j (c i) -> p e c j i", i=4),
+            )
+
+        def quantize_w2(g, experts):
+            e0, e1 = experts
+            flat = "p e c -> p (e c)"
+            quantize(
+                w2_codes[:, g, e0:e1, :].rearrange(flat),
+                w2_scales[:, g, e0:e1, :].rearrange(flat),
+                w2_rounded[:, g, e0:e1, :].rearrange(flat),
+            )
+
+        def multiply_w2(g, experts):
+            e0, e1 = experts
+            bank = psum.tile([P, e1 - e0, C], F32, name="y_bank", bufs=Y_BANKS)
+            for e in range(e0, e1):
+                multiply(
+                    bank[:, e - e0, :],
+                    w2_codes[:, g, e, :],
+                    w2_scales[:, g, e, :],
+                    h_quantized[e][0][:],
+                    h_quantized[e][1][:],
+                    True,
+                    True,
+                )
+            y_banks[(g, e0)] = bank
+
+        def empty_y(g, experts):
+            e0, e1 = experts
+            nc.scalar.copy(out=y_sb[g][:, e0 * C : e1 * C], in_=y_banks[(g, e0)][:].rearrange("p e s -> p (e s)"))
+
+        def finish_y(g, experts):
+            quantize_w2(g, experts)
+            multiply_w2(g, experts)
+            empty_y(g, experts)
+
+        def combine(g):
+            for (lo, hi), on_gpsimd in COMBINE_PLAN[g]:
+                first = raw_tile([P, hi - lo], "first")
+                second = raw_tile([P, hi - lo], "second")
+                total = raw_tile([P, hi - lo], "total")
+                nc.vector.tensor_copy(first[:], y_sb[g][:].indirect(pos1_sb[:, list_columns(lo, hi)]))
+                nc.vector.tensor_copy(second[:], y_sb[g][:].indirect(pos2_sb[:, list_columns(lo, hi)]))
+                adder = nc.gpsimd if on_gpsimd else nc.vector
+                adder.tensor_tensor(total[:], first[:], second[:], ADD)
                 nc.sync.dma_start(out=out[g * P : (g + 1) * P, lo:hi], in_=total[:])
+
+        gather_x(0, 0)
+        round_x(0, 0, S // 2, False)
+        gather_x(0, 1)
+        gather_x(1, 0)
+        gather_x(1, 1)
+        for a, lo, hi, on_vector in X_ROUND:
+            round_x(a, lo, hi, on_vector)
+        round_w2(0, EARLY, True)
+        for a in reversed(range(PASSES)):
+            for lo, hi in X_QUANTISE[a]:
+                quantize_x(a, lo, hi)
+
+        early_step = 2 * (EARLY[1] - 1) + HIDDEN_LAG
+        for step in range(MATRICES + HIDDEN_LAG - 1):
+            if step < MATRICES:
+                round_chunk(step, 0)
+            if step == SPLIT_MATRIX + 1:
+                quantize_w2(0, EARLY)
+            if step >= HIDDEN_LAG and step % 2 == 0:
+                make_hidden((step - HIDDEN_LAG) // 2)
+            if step == early_step:
+                multiply_w2(0, EARLY)
+            if 1 <= step <= MATRICES:
+                quantize_matrix(step - 1, 1 if step - 1 == SPLIT_MATRIX else 0, PASSES)
+                multiply_matrix(step - 1)
+            if step < MATRICES:
+                round_chunk(step, 1)
+            if step == SPLIT_MATRIX:
+                quantize_matrix(step, 0, 1)
+            if step == early_step:
+                empty_y(0, EARLY)
+            if SILU_LAG <= step < MATRICES + SILU_LAG and step % 2 == 0:
+                activate((step - SILU_LAG) // 2)
+
+        round_w2(0, MIDDLE, False)
+        finish_y(0, MIDDLE)
+        round_w2(0, LAST, True)
+        round_w2(1, MIDDLE, False)
+        round_w2(1, LAST, True)
+        finish_y(0, LAST)
+        combine(0)
+        finish_y(1, MIDDLE)
+        finish_y(1, LAST)
+        round_w2(1, EARLY, False)
+        finish_y(1, EARLY)
+        combine(1)

from contextlib import ExitStack

import concourse.mybir as mybir

K, T, E, C, H, N = 1024, 640, 5, 256, 512, 256
S = E * C
P = 128
PACK = 4
K_PASS = P * PACK
PASSES = K // K_PASS
MATRICES = 2 * E
BANK_SLOTS = 128
LIST_ROWS = 16

FLOPS = 2 * S * (2 * K * H + H * N)
BYTES = 4 * (K * T + E * (2 * K * H + H * N) + S + N * T) + 2 * P * (S + 2 * T) // LIST_ROWS

WINDOW = T + 32
SLOT_HALVES = ((0, S // 2), (S // 2, S))
TAIL_SLOT = S - BANK_SLOTS
X_ROUND = ((0, TAIL_SLOT, S, True), (1, 0, S // 2, True), (1, S // 2, S, True), (0, S // 2, TAIL_SLOT, False))
X_QUANTISE = (((0, 4 * C), (4 * C, S)), ((0, C), (C, S)))
CHUNKS_BEFORE_TOKENS = (0, 0, 0, 3, 4, 4, 4, 11)
VECTOR_HALVES = {(1, 1): 1, (5, 1): 1, (6, 0): 2, (7, 1): 2, (8, 0): 2, (9, 1): 2}
SPLIT_MATRIX = 1
CHUNKS_BEFORE_POS = 13
SILU_LAG = 4
HIDDEN_LAG = 6
EARLY, MIDDLE, LAST = (0, 2), (2, 4), (4, 5)
COMBINE_PLAN = (
    (((0, T), True),),
    (((0, T // 2), True), ((T // 2, T), False)),
)

RAW_BUFS = 7
PICKED_BUFS = 2
ROUNDED_BUFS = 3
CODE_BUFS = 4
SILU_BUFS = 6
H_BUFS = 2
FIRST_BANKS = 3
Y_BANKS = 2

F32 = mybir.dt.float32
BF16 = mybir.dt.bfloat16
U32 = mybir.dt.uint32
U16 = mybir.dt.uint16
U8 = mybir.dt.uint8
FP8X4 = mybir.dt.float8_e4m3fn_x4
MULT = mybir.AluOpType.mult
ADD = mybir.AluOpType.add
SILU = mybir.ActivationFunctionType.Silu


def tile_moe_pre_glu_silu_kernel(tc, xT, w1, w3, w2, gate, offs, pos1, pos2, out):
    nc = tc.nc

    def round_copy(on_vector, dst, src):
        if on_vector:
            nc.vector.tensor_copy(out=dst, in_=src)
        else:
            nc.scalar.copy(out=dst, in_=src)

    def quantize(codes, scales, values):
        nc.vector.quantize_mx(out=codes.bitcast(FP8X4), scales=scales, in_=values)

    def multiply(bank, stationary, stationary_scales, moving, moving_scales, start, stop):
        nc.tensor.matmul_mx(
            out=bank,
            lhsT=stationary.bitcast(FP8X4),
            lhsT_scale=stationary_scales,
            rhs=moving.bitcast(FP8X4),
            rhs_scale=moving_scales,
            start=start,
            stop=stop,
        )

    def list_columns(lo, hi):
        return slice(lo // LIST_ROWS, hi // LIST_ROWS)

    with ExitStack() as ctx:
        keep = ctx.enter_context(tc.tile_pool(name="keep", bufs=1))
        ring = ctx.enter_context(tc.tile_pool(name="ring", bufs=1))
        psum = ctx.enter_context(tc.psum_pool(name="psum", bufs=1))

        offs_sb = keep.tile([P, S // LIST_ROWS], U16, name="offs_sb")
        pos1_sb = keep.tile([P, T // LIST_ROWS], U16, name="pos1_sb")
        pos2_sb = keep.tile([P, T // LIST_ROWS], U16, name="pos2_sb")
        gate_sb = [keep.tile([P, hi - lo], F32, name=f"gate{lo}") for lo, hi in SLOT_HALVES]
        tokens = [keep.tile([P, WINDOW], F32, name=f"tokens{tile}") for tile in range(PASSES * PACK)]
        x_rounded = keep.tile([P, PASSES, PACK * S], BF16, name="x_rounded", align_bytes=64)
        x_codes = keep.tile([P, PASSES, S], U32, name="x_codes", align_bytes=64)
        x_scales = keep.tile([P, PASSES, S], U8, name="x_scales", align_bytes=64)
        w2_rounded = keep.tile([P, N // P, E, PACK * P], BF16, name="w2_rounded", align_bytes=64)
        w2_codes = keep.tile([P, N // P, E, P], U32, name="w2_codes", align_bytes=64)
        w2_scales = keep.tile([P, N // P, E, P], U8, name="w2_scales", align_bytes=64)
        y_sb = [keep.tile([P, S], F32, name=f"y_sb{g}") for g in range(N // P)]

        def raw_tile(shape, name):
            return ring.tile(shape, F32, name=name, tag="raw", bufs=RAW_BUFS)

        for tile in tokens:
            nc.gpsimd.memset(tile[:, T:WINDOW], 0.0)
        token_rows = xT.rearrange("(a p j) t -> a j p t", p=P, j=PACK)
        chunks = [(matrix, a) for matrix in range(MATRICES) for a in range(PASSES)]
        w_raw = {}

        def load_tokens(tile):
            nc.sync.dma_start(out=tokens[tile][:, 0:T], in_=token_rows[tile // PACK, tile % PACK])

        load_tokens(0)
        nc.sync.dma_start(out=offs_sb[:], in_=offs)
        for half, (lo, hi) in reversed(list(enumerate(SLOT_HALVES))):
            nc.sync.dma_start(out=gate_sb[half][:], in_=gate[0:P, lo:hi])
        for loaded, (matrix, a) in enumerate(chunks):
            for tile in range(1, PASSES * PACK):
                if CHUNKS_BEFORE_TOKENS[tile] == loaded:
                    load_tokens(tile)
            if loaded == CHUNKS_BEFORE_POS:
                nc.sync.dma_start(out=pos1_sb[:], in_=pos1)
                nc.sync.dma_start(out=pos2_sb[:], in_=pos2)
            rows = (w1, w3)[matrix % 2][matrix // 2, a * K_PASS : (a + 1) * K_PASS, :]
            w_raw[(matrix, a)] = raw_tile([P, PACK, H], "w_raw")
            nc.sync.dma_start(out=w_raw[(matrix, a)][:], in_=rows.rearrange("(p j) c -> p j c", j=PACK))
        w2_raw = {}
        for e0, e1 in (EARLY, MIDDLE, LAST):
            w2_raw[e0] = raw_tile([P, e1 - e0, PACK, N], "w2_raw")
            nc.sync.dma_start(out=w2_raw[e0][:], in_=w2[e0:e1].rearrange("e (p j) c -> p e j c", j=PACK))

        picked = {}

        def gather_x(a, half):
            lo, hi = SLOT_HALVES[half]
            picked[(a, half)] = ring.tile([P, PACK, hi - lo], F32, name="picked", bufs=PICKED_BUFS)
            for j in range(PACK):
                window = tokens[a * PACK + j][:].indirect(offs_sb[:, list_columns(lo, hi)])
                nc.vector.tensor_tensor(picked[(a, half)][:, j, :], window, gate_sb[half][:], MULT)

        def round_x(a, lo, hi, on_vector):
            half = lo // (S // 2)
            base = SLOT_HALVES[half][0]
            round_copy(
                on_vector,
                x_rounded[:, a, PACK * lo : PACK * hi].rearrange("p (c i j) -> p c j i", i=4, j=PACK),
                picked[(a, half)][:, :, lo - base : hi - base].rearrange("p j (c i) -> p c j i", i=4),
            )

        def quantize_x(a, lo, hi):
            quantize(x_codes[:, a, lo:hi], x_scales[:, a, lo:hi], x_rounded[:, a, PACK * lo : PACK * hi])

        w_rounded = {}
        w_quantized = {}
        banks = {}
        activated = {}
        h_quantized = {}

        def round_chunk(matrix, a):
            if a == 0:
                w_rounded[matrix] = ring.tile(
                    [P, PASSES, PACK * H], BF16, name="w_rounded", bufs=ROUNDED_BUFS, align_bytes=64
                )
            dst = w_rounded[matrix][:, a, :].rearrange("p (u q j) -> p q j u", u=PACK, j=PACK)
            src = w_raw[(matrix, a)][:].rearrange("p j (q u) -> p q j u", u=PACK)
            split = P - VECTOR_HALVES.get((matrix, a), 0) * P // 2
            if split > 0:
                round_copy(False, dst[:, 0:split], src[:, 0:split])
            if split < P:
                round_copy(True, dst[:, split:P], src[:, split:P])

        def quantize_matrix(matrix, a0, a1):
            if a0 == 0:
                codes = ring.tile([P, PASSES, H], U32, name="w_codes", bufs=CODE_BUFS, align_bytes=64)
                scales = ring.tile([P, PASSES, H], U8, name="w_scales", bufs=CODE_BUFS, align_bytes=64)
                w_quantized[matrix] = (codes, scales)
            codes, scales = w_quantized[matrix]
            flat = "p a c -> p (a c)"
            quantize(
                codes[:, a0:a1, :].rearrange(flat),
                scales[:, a0:a1, :].rearrange(flat),
                w_rounded[matrix][:, a0:a1, :].rearrange(flat),
            )

        def multiply_matrix(matrix):
            codes, scales = w_quantized[matrix]
            for part in range(C // BANK_SLOTS):
                bank = psum.tile([P, PACK, BANK_SLOTS], F32, name=f"first_bank{matrix % 2}", bufs=FIRST_BANKS)
                banks[(matrix, part)] = bank
                first_slot = (matrix // 2) * C + part * BANK_SLOTS
                slots = slice(first_slot, first_slot + BANK_SLOTS)
                for u in range(PACK):
                    cols = slice(u * P, (u + 1) * P)
                    for a in range(PASSES):
                        multiply(
                            bank[:, u, :],
                            codes[:, a, cols],
                            scales[:, a, cols],
                            x_codes[:, a, slots],
                            x_scales[:, a, slots],
                            a == 0,
                            a == PASSES - 1,
                        )

        def activate(e):
            for part in range(C // BANK_SLOTS):
                silu = ring.tile([P, BANK_SLOTS, PACK], F32, name="silu", bufs=SILU_BUFS)
                nc.scalar.activation(out=silu[:], in_=banks[(2 * e, part)][:].rearrange("p u s -> p s u"), func=SILU)
                activated[(e, part)] = silu

        def make_hidden(e):
            h = ring.tile([P, C, PACK], BF16, name="h", bufs=H_BUFS, align_bytes=64)
            for part in range(C // BANK_SLOTS):
                nc.vector.tensor_tensor(
                    h[:, part * BANK_SLOTS : (part + 1) * BANK_SLOTS, :],
                    banks[(2 * e + 1, part)][:].rearrange("p u s -> p s u"),
                    activated[(e, part)][:],
                    MULT,
                )
            codes = ring.tile([P, C], U32, name="h_codes", bufs=E, align_bytes=64)
            scales = ring.tile([P, C], U8, name="h_scales", bufs=E, align_bytes=64)
            quantize(codes[:], scales[:], h[:].rearrange("p s u -> p (s u)"))
            h_quantized[e] = (codes, scales)

        y_banks = {}

        def round_w2(g, experts, on_vector):
            e0, e1 = experts
            round_copy(
                on_vector,
                w2_rounded[:, g, e0:e1, :].rearrange("p e (c i j) -> p e c j i", i=4, j=PACK),
                w2_raw[e0][:, :, :, g * P : (g + 1) * P].rearrange("p e j (c i) -> p e c j i", i=4),
            )

        def quantize_w2(g, experts):
            e0, e1 = experts
            flat = "p e c -> p (e c)"
            quantize(
                w2_codes[:, g, e0:e1, :].rearrange(flat),
                w2_scales[:, g, e0:e1, :].rearrange(flat),
                w2_rounded[:, g, e0:e1, :].rearrange(flat),
            )

        def multiply_w2(g, experts):
            e0, e1 = experts
            bank = psum.tile([P, e1 - e0, C], F32, name="y_bank", bufs=Y_BANKS)
            for e in range(e0, e1):
                multiply(
                    bank[:, e - e0, :],
                    w2_codes[:, g, e, :],
                    w2_scales[:, g, e, :],
                    h_quantized[e][0][:],
                    h_quantized[e][1][:],
                    True,
                    True,
                )
            y_banks[(g, e0)] = bank

        def empty_y(g, experts):
            e0, e1 = experts
            nc.scalar.copy(out=y_sb[g][:, e0 * C : e1 * C], in_=y_banks[(g, e0)][:].rearrange("p e s -> p (e s)"))

        def finish_y(g, experts):
            quantize_w2(g, experts)
            multiply_w2(g, experts)
            empty_y(g, experts)

        def combine(g):
            for (lo, hi), on_gpsimd in COMBINE_PLAN[g]:
                first = raw_tile([P, hi - lo], "first")
                second = raw_tile([P, hi - lo], "second")
                total = raw_tile([P, hi - lo], "total")
                nc.vector.tensor_copy(first[:], y_sb[g][:].indirect(pos1_sb[:, list_columns(lo, hi)]))
                nc.vector.tensor_copy(second[:], y_sb[g][:].indirect(pos2_sb[:, list_columns(lo, hi)]))
                adder = nc.gpsimd if on_gpsimd else nc.vector
                adder.tensor_tensor(total[:], first[:], second[:], ADD)
                nc.sync.dma_start(out=out[g * P : (g + 1) * P, lo:hi], in_=total[:])

        gather_x(0, 0)
        round_x(0, 0, S // 2, False)
        gather_x(0, 1)
        gather_x(1, 0)
        gather_x(1, 1)
        for a, lo, hi, on_vector in X_ROUND:
            round_x(a, lo, hi, on_vector)
        round_w2(0, EARLY, True)
        for a in reversed(range(PASSES)):
            for lo, hi in X_QUANTISE[a]:
                quantize_x(a, lo, hi)

        early_step = 2 * (EARLY[1] - 1) + HIDDEN_LAG
        for step in range(MATRICES + HIDDEN_LAG - 1):
            if step < MATRICES:
                round_chunk(step, 0)
            if step == SPLIT_MATRIX + 1:
                quantize_w2(0, EARLY)
            if step >= HIDDEN_LAG and step % 2 == 0:
                make_hidden((step - HIDDEN_LAG) // 2)
            if step == early_step:
                multiply_w2(0, EARLY)
            if 1 <= step <= MATRICES:
                quantize_matrix(step - 1, 1 if step - 1 == SPLIT_MATRIX else 0, PASSES)
                multiply_matrix(step - 1)
            if step < MATRICES:
                round_chunk(step, 1)
            if step == SPLIT_MATRIX:
                quantize_matrix(step, 0, 1)
            if step == early_step:
                empty_y(0, EARLY)
            if SILU_LAG <= step < MATRICES + SILU_LAG and step % 2 == 0:
                activate((step - SILU_LAG) // 2)

        round_w2(0, MIDDLE, False)
        finish_y(0, MIDDLE)
        round_w2(0, LAST, True)
        round_w2(1, MIDDLE, False)
        round_w2(1, LAST, True)
        finish_y(0, LAST)
        combine(0)
        finish_y(1, MIDDLE)
        finish_y(1, LAST)
        round_w2(1, EARLY, False)
        finish_y(1, EARLY)
        combine(1)
